import numpy as np
import ml_dtypes


def mxq(x, axis, fmt="e4m3"):
    dtype, down = {"e4m3": (ml_dtypes.float8_e4m3fn, 7), "e5m2": (ml_dtypes.float8_e5m2, 14)}[fmt]
    v = np.moveaxis(np.asarray(x, np.float32).astype(ml_dtypes.bfloat16).astype(np.float64), axis, -1)
    blocks = v.reshape(v.shape[:-1] + (-1, 32))
    amax = np.abs(blocks).max(-1, keepdims=True)
    byte = np.maximum(np.where(amax > 0, np.frexp(amax)[1] - 1 + 127, 0) - down, 1)
    scale = np.exp2(byte - 127.0)
    codes = (blocks / scale).astype(np.float32).astype(dtype).astype(np.float64)
    return np.moveaxis((codes * scale).reshape(v.shape), -1, axis)


WIDE = False


def mx_kscale(k):
    if not WIDE:
        return np.ones(k)
    levels = np.array([24, -24, 12, -12, 0])
    if k % 512:
        return np.exp2(np.random.permutation(np.resize(levels, k // 32))).repeat(32)
    a = np.empty((k // 512, 16))
    for p in range(k // 512):
        a[p, :8] = np.random.permutation(np.resize(levels, 8))
        for g in range(8):
            far = levels[np.abs(levels - a[p, g]) >= 10]
            a[p, g + 8] = far[np.random.randint(len(far))]
    return np.exp2(a.ravel()).repeat(32)


def f64(x):
    return np.asarray(x).astype(np.float64)


def striped(idx):
    return np.tile(idx.reshape(-1, 16).T, (8, 1)).astype(np.uint16)


def unstriped(offs):
    return offs[:16].T.reshape(-1).astype(np.int64)


E2M1 = np.array([0.0, 0.5, 1.0, 1.5, 2.0, 3.0, 4.0, 6.0, -0.0, -0.5, -1.0, -1.5, -2.0, -3.0, -4.0, -6.0])


def pack_weight(w, fmt):
    k, n = w.shape
    w = f64(np.asarray(w, np.float32).astype(ml_dtypes.bfloat16)).reshape(k // 32, 32, n)
    amax = np.abs(w).max(1)
    if fmt == "e4m3":
        byte = np.frexp(amax)[1] - 1 + 127 - 7
    else:
        mant, ex = np.frexp(amax / 6.0)
        byte = np.where(mant > 0.5, ex, ex - 1) + 127
    byte = np.clip(np.where(amax > 0, byte, 1), 1, 254)
    scaled = (w * np.exp2(127.0 - byte)[:, None, :]).reshape(k, n).astype(np.float32)
    by_word = np.ascontiguousarray(scaled.reshape(k // 512, 128, 4, n).transpose(0, 1, 3, 2))
    if fmt == "e4m3":
        words = by_word.astype(ml_dtypes.float8_e4m3fn).view(np.uint8)
    else:
        c = by_word.astype(ml_dtypes.float4_e2m1fn).view(np.uint8) & 0xF
        words = (c[..., 0::2] | (c[..., 1::2] << 4)).reshape(k // 512, 128, 2 * n)
    return np.ascontiguousarray(words), np.ascontiguousarray(byte.astype(np.uint8).reshape(k // 512, 16, n))


def unpack_weight(words, scales, fmt):
    g, _, n = scales.shape
    words = np.ascontiguousarray(words).reshape(g, 128, n, -1)
    if fmt == "e4m3":
        vals = words.view(ml_dtypes.float8_e4m3fn).astype(np.float64)
    else:
        nib = np.empty((g, 128, n, 4), np.uint8)
        nib[..., 0::2] = words & 0xF
        nib[..., 1::2] = words >> 4
        vals = E2M1[nib]
    vals = vals * np.repeat(np.exp2(scales.astype(np.float64) - 127.0), 8, axis=1)[..., None]
    return vals.transpose(0, 1, 3, 2).reshape(g * 512, n)


def pack_table4(v):
    words, scales = pack_weight(v, "e2m1")
    g, t = words.shape[0] // 2, v.shape[1]
    return np.ascontiguousarray(words.reshape(g, 2, 128, t, 2).transpose(0, 2, 3, 1, 4).reshape(g, 128, t, 4)), scales


def unpack_table4(words, scales):
    g, _, t, _ = words.shape
    return unpack_weight(words.reshape(g, 128, t, 2, 2).transpose(0, 3, 1, 2, 4).reshape(2 * g, 128, 2 * t), scales, "e2m1")


K, R, N, T, J = 1024, 512, 256, 4096, 512


def setup_inputs():
    n = np.random.standard_normal
    s = mx_kscale(K)[:, None]
    u = mx_kscale(R)[:, None]
    p_tab = pack_table4(n((K, T)) * s)
    p_w = pack_weight(n((K, R)) / np.sqrt(K) / s * u.T, "e2m1")
    p_wd = pack_weight(n((R, N)) / np.sqrt(R) / u, "e4m3")
    return {
        "tab_words": p_tab[0],
        "tab_scales": p_tab[1],
        "c": (n((K, J)) * s).astype(np.float32),
        "w_words": p_w[0],
        "w_scales": p_w[1],
        "wc": (n((K, R)) / np.sqrt(K) / s * u.T).astype(np.float32),
        "wd_words": p_wd[0],
        "wd_scales": p_wd[1],
        "gm": (n((N, J))).astype(np.float32),
        "offs": striped(np.concatenate([np.random.permutation(T)[:J] for _ in range(3)])),
    }


def reference(tab_words, tab_scales, c, w_words, w_scales, wc, wd_words, wd_scales, gm, offs):
    idx = unstriped(offs).reshape(3, J)
    tab_ = unpack_table4(tab_words, tab_scales)[:, idx]
    c_ = mxq(f64(c), 0, "e4m3")
    w_ = unpack_weight(w_words, w_scales, "e2m1")
    a0 = w_.T @ tab_[:, 0]
    a1 = w_.T @ tab_[:, 1]
    a2 = w_.T @ tab_[:, 2]
    wc_ = mxq(f64(wc), 0, "e4m3")
    ac = wc_.T @ c_
    h = np.maximum(np.maximum(np.maximum(a0, a1), a2) + ac, 0.0)
    h_ = mxq(h, 0, "e4m3")
    wd_ = unpack_weight(wd_words, wd_scales, "e4m3")
    y = wd_.T @ h_
    return y * f64(gm)

@@ -1,0 +1,256 @@
+from contextlib import ExitStack
+
+import concourse.mybir as mybir
+
+K, R, N, T, J = 1024, 512, 256, 4096, 512
+LISTS = 3
+FLOPS = 2 * (LISTS + 1) * K * R * J + 2 * R * N * J
+
+F32 = mybir.dt.float32
+BF16 = mybir.dt.bfloat16
+I32 = mybir.dt.int32
+U32 = mybir.dt.uint32
+U16 = mybir.dt.uint16
+U8 = mybir.dt.uint8
+FP8X4 = mybir.dt.float8_e4m3fn_x4
+FP4X4 = mybir.dt.float4_e2m1fn_x4
+ALU = mybir.AluOpType
+ACT = mybir.ActivationFunctionType
+
+P = 128
+PACK = 4
+PASSES = K // (P * PACK)
+QUADS = 4
+JQ = 128
+PARTS = J // JQ
+
+
+def load_scale_rows(queue, plane, scales):
+    for q in range(QUADS):
+        queue.dma_start(
+            out=plane[32 * q : 32 * q + 4, :, :].bitcast(I32),
+            in_=scales[:, 4 * q : 4 * q + 4, :].rearrange("a r n -> r a n").bitcast(I32),
+        )
+
+
+def tile_list_pnet_gate_kernel(
+    tc, tab_words, tab_scales, c, w_words, w_scales, wc, wd_words, wd_scales, gm, offs, out
+):
+    nc = tc.nc
+    with ExitStack() as ctx:
+        keep = ctx.enter_context(tc.tile_pool(name="keep", bufs=1))
+        psum = ctx.enter_context(tc.psum_pool(name="psum", bufs=1))
+
+        offsets = keep.tile([P, LISTS * J // 16], U16, name="offsets")
+        nc.sync.dma_start(offsets[:], offs)
+
+        tab_s = keep.tile([P, T], U8, name="tab_s", tag="reuse", align_bytes=64)
+        v_s1 = keep.tile([P, LISTS * J], U8, name="v_s1", align_bytes=64)
+        w_s_raw = keep.tile([P, PASSES, R], U8, name="w_s_raw", align_bytes=64)
+        wd_s = keep.tile([P, 1, N], U8, name="wd_s", align_bytes=64)
+        nc.vector.memset(tab_s[:].bitcast(I32), 0)
+        nc.gpsimd.memset(w_s_raw[:].bitcast(I32), 0)
+        nc.vector.memset(v_s1[:].bitcast(I32), 0)
+        nc.vector.memset(wd_s[:].bitcast(I32), 0)
+
+        warm = keep.tile([P, 2], F32, name="warm")
+        nc.vector.memset(warm[:, 0:1], 0.0)
+        nc.scalar.activation(out=warm[:, 1:2], in_=warm[:, 0:1], func=ACT.Relu)
+
+        nc.sync.dma_start(out=tab_s[16:32, :].bitcast(I32), in_=tab_scales[1].bitcast(I32))
+        for q in range(QUADS):
+            nc.sync.dma_start(
+                out=tab_s[32 * q : 32 * q + 4, :].bitcast(I32),
+                in_=tab_scales[0, 4 * q : 4 * q + 4, :].bitcast(I32),
+            )
+        tab_w = keep.tile([P, T], I32, name="tab_w", align_bytes=64)
+        nc.sync.dma_start(out=tab_w[:], in_=tab_words[0].rearrange("p t b -> p (t b)").bitcast(I32))
+        w_w_raw = keep.tile([P, PASSES, 2 * R], U8, name="w_w_raw", align_bytes=64)
+        nc.sync.dma_start(out=w_w_raw[:].bitcast(I32), in_=w_words.rearrange("a p n -> p a n").bitcast(I32))
+        load_scale_rows(nc.gpsimd, w_s_raw, w_scales)
+
+        wc_raw = [keep.tile([P, PACK, R], F32, name=f"wc_raw{a}") for a in range(PASSES)]
+
+        def load_rows(raw, src, a):
+            rows = src[a * P * PACK : (a + 1) * P * PACK, :]
+            nc.sync.dma_start(out=raw[:], in_=rows.rearrange("(p i) n -> p i n", i=PACK))
+
+        for a in range(PASSES):
+            load_rows(wc_raw[a], wc, a)
+
+        v_s0 = keep.tile([P, LISTS * J], U8, name="v_s0", align_bytes=64)
+        nc.vector.tensor_copy(v_s0[:], tab_s[:].indirect(offsets[:]))
+        for q in range(QUADS):
+            nc.scalar.dma_start(
+                out=v_s1[32 * q : 32 * q + 4, :].bitcast(I32),
+                in_=v_s0[16 + 4 * q : 20 + 4 * q, :].bitcast(I32),
+            )
+        v_s = (v_s0, v_s1)
+
+        c_raw = [
+            keep.tile([P, PACK, J], F32, name="c_raw0", tag="reuse", align_bytes=64),
+            keep.tile([P, PACK, J], F32, name="c_raw1"),
+        ]
+        for a in range(PASSES):
+            load_rows(c_raw[a], c, a)
+        wd_w = keep.tile([P, N], I32, name="wd_w", align_bytes=64)
+        nc.sync.dma_start(out=wd_w[:], in_=wd_words[0].rearrange("p n b -> p (n b)").bitcast(I32))
+        gate = keep.tile([P, N // P, J], F32, name="gate")
+        nc.sync.dma_start(out=gate[:], in_=gm.rearrange("(u p) j -> p u j", p=P))
+        load_scale_rows(nc.sync, wd_s, wd_scales)
+
+        v_pair = [keep.tile([P, J], U32, name=f"v_pair{g}", align_bytes=64) for g in range(LISTS)]
+        v_w = [keep.tile([P, PASSES, 2 * J], U8, name=f"v_w{g}", align_bytes=64) for g in range(LISTS)]
+
+        def picks(g):
+            return offsets[:, g * J // 16 : (g + 1) * J // 16]
+
+        def gather_words(g):
+            nc.vector.tensor_copy(v_pair[g][:], tab_w[:].bitcast(U32).indirect(picks(g)))
+
+        def part_words(g):
+            nc.vector.tensor_copy(
+                v_w[g][:].bitcast(U16), v_pair[g][:].bitcast(U16).rearrange("p (j a) -> p a j", a=PASSES)
+            )
+
+        w_w = keep.tile([P, PASSES, 2 * R], U8, name="w_w", align_bytes=64)
+        w_s = keep.tile([P, PASSES, R], U8, name="w_s", align_bytes=64)
+
+        def permute_w():
+            nc.vector.tensor_copy(
+                w_s[:].rearrange("p a (t m) -> p a t m", t=PACK),
+                w_s_raw[:].rearrange("p a (m t) -> p a t m", t=PACK),
+            )
+            nc.vector.tensor_copy(
+                w_w[:].bitcast(U16).rearrange("p a (t m) -> p a t m", t=PACK),
+                w_w_raw[:].bitcast(U16).rearrange("p a (m t) -> p a t m", t=PACK),
+            )
+
+        def neighbour_sums(g, tag):
+            banks = []
+            for t in range(PACK):
+                bank = psum.tile([P, J], F32, name=f"a{g}_{t}", tag=f"{tag}{t}")
+                for a in range(PASSES):
+                    nc.tensor.matmul_mx(
+                        out=bank[:],
+                        lhsT=w_w[:, a, 2 * P * t : 2 * P * (t + 1)].bitcast(FP4X4),
+                        lhsT_scale=w_s[:, a, P * t : P * (t + 1)],
+                        rhs=v_w[g][:, a, :].bitcast(FP4X4),
+                        rhs_scale=v_s[a][:, g * J : (g + 1) * J],
+                        start=(a == 0),
+                        stop=(a == PASSES - 1),
+                    )
+                banks.append(bank)
+            return banks
+
+        wc_bf = [keep.tile([P, PACK * R], BF16, name=f"wc_bf{a}", align_bytes=64) for a in range(PASSES)]
+        c_bf = [keep.tile([P, PACK * J], BF16, name=f"c_bf{a}", align_bytes=64) for a in range(PASSES)]
+        wc_w = [keep.tile([P, R], U32, name=f"wc_w{a}", align_bytes=64) for a in range(PASSES)]
+        wc_s = [keep.tile([P, R], U8, name=f"wc_s{a}", align_bytes=64) for a in range(PASSES)]
+        c_w = [keep.tile([P, J], U32, name=f"c_w{a}", align_bytes=64) for a in range(PASSES)]
+        c_s = [keep.tile([P, J], U8, name=f"c_s{a}", align_bytes=64) for a in range(PASSES)]
+
+        def round_wc(a):
+            nc.scalar.copy(
+                out=wc_bf[a][:].rearrange("p (t m i) -> p m i t", t=PACK, i=PACK),
+                in_=wc_raw[a][:].rearrange("p i (m t) -> p m i t", t=PACK),
+            )
+
+        def round_c(a, j0, j1):
+            nc.scalar.copy(
+                out=c_bf[a][:, PACK * j0 : PACK * j1].rearrange("p (b e i) -> p b i e", e=4, i=PACK),
+                in_=c_raw[a][:, :, j0:j1].rearrange("p i (b e) -> p b i e", e=4),
+            )
+
+        def quantize_wc(a):
+            nc.vector.quantize_mx(out=wc_w[a][:].bitcast(FP8X4), scales=wc_s[a][:], in_=wc_bf[a][:])
+
+        def quantize_c(a, j0, j1):
+            nc.vector.quantize_mx(
+                out=c_w[a][:, j0:j1].bitcast(FP8X4),
+                scales=c_s[a][:, j0:j1],
+                in_=c_bf[a][:, PACK * j0 : PACK * j1],
+            )
+
+        permute_w()
+        gather_words(0)
+        part_words(0)
+        a0 = neighbour_sums(0, "x")
+        gather_words(1)
+        part_words(1)
+        a1 = neighbour_sums(1, "y")
+        gather_words(2)
+        part_words(2)
+
+        round_wc(0)
+        first = keep.tile([P, PACK, J], F32, name="first")
+        for t in range(PACK):
+            nc.scalar.copy(out=first[:, t, :], in_=a0[t][:])
+        a2 = neighbour_sums(2, "x")
+        round_wc(1)
+        quantize_wc(0)
+        second = keep.tile([P, PACK, J], F32, name="second")
+        for t in range(PACK):
+            nc.vector.tensor_tensor(second[:, t, :], a1[t][:], first[:, t, :], ALU.max)
+        for j0 in range(0, J, 256):
+            nc.gpsimd.tensor_scalar(
+                c_bf[0][:, PACK * j0 : PACK * (j0 + 256)].rearrange("p (j i) -> p j i", i=PACK),
+                c_raw[0][:, :, j0 : j0 + 256].rearrange("p i j -> p j i"),
+                1.0,
+                0.0,
+                ALU.mult,
+                ALU.add,
+            )
+        quantize_wc(1)
+        pooled = keep.tile([P, PACK, J], F32, name="pooled")
+        for t in range(PACK):
+            nc.vector.tensor_tensor(pooled[:, t, :], a2[t][:], second[:, t, :], ALU.max)
+        quantize_c(0, 0, J)
+
+        own = []
+        for q in range(PARTS):
+            j0, j1 = q * JQ, (q + 1) * JQ
+            round_c(1, j0, j1)
+            quantize_c(1, j0, j1)
+            bank = psum.tile([P, PACK, JQ], F32, name=f"own{q}", tag=f"y{q}")
+            for t in range(PACK):
+                for a in range(PASSES):
+                    nc.tensor.matmul_mx(
+                        out=bank[:, t, :],
+                        lhsT=wc_w[a][:, P * t : P * (t + 1)].bitcast(FP8X4),
+                        lhsT_scale=wc_s[a][:, P * t : P * (t + 1)],
+                        rhs=c_w[a][:, j0:j1].bitcast(FP8X4),
+                        rhs_scale=c_s[a][:, j0:j1],
+                        start=(a == 0),
+                        stop=(a == PASSES - 1),
+                    )
+            own.append(bank)
+
+        out_rows = out.rearrange("(u p) j -> p u j", p=P)
+        for q in range(PARTS):
+            j0, j1 = q * JQ, (q + 1) * JQ
+            pre = keep.tile([P, PACK, JQ], F32, name=f"pre{q}")
+            nc.vector.tensor_tensor(pre[:], own[q][:], pooled[:, :, j0:j1], ALU.add)
+            h_bf = keep.tile([P, PACK * JQ], BF16, name=f"h_bf{q}", align_bytes=64)
+            nc.scalar.activation(
+                out=h_bf[:].rearrange("p (b e t) -> p b t e", e=4, t=PACK),
+                in_=pre[:].rearrange("p t (b e) -> p b t e", e=4),
+                func=ACT.Relu,
+            )
+            h_w = keep.tile([P, JQ], U32, name=f"h_w{q}", align_bytes=64)
+            h_s = keep.tile([P, JQ], U8, name=f"h_s{q}", align_bytes=64)
+            nc.vector.quantize_mx(out=h_w[:].bitcast(FP8X4), scales=h_s[:], in_=h_bf[:])
+            bank = psum.tile([P, N // P, JQ], F32, name=f"y{q}", tag=f"x{q}")
+            for u in range(N // P):
+                nc.tensor.matmul_mx(
+                    out=bank[:, u, :],
+                    lhsT=wd_w[:, P * u : P * (u + 1)].bitcast(FP8X4),
+                    lhsT_scale=wd_s[:, 0, P * u : P * (u + 1)],
+                    rhs=h_w[:].bitcast(FP8X4),
+                    rhs_scale=h_s[:],
+                    start=True,
+                    stop=True,
+                )
+            res = keep.tile([P, N // P, JQ], F32, name=f"res{q}")
+            nc.vector.tensor_tensor(res[:], bank[:], gate[:, :, j0:j1], ALU.mult)
+            nc.sync.dma_start(out=out_rows[:, :, j0:j1], in_=res[:])

@@ -44,62 +44,47 @@ def tile_list_pnet_gate_kernel(
         offsets = keep.tile([P, LISTS * J // 16], U16, name="offsets")
         nc.sync.dma_start(offsets[:], offs)
 
-        tab_s = keep.tile([P, T], U8, name="tab_s", tag="reuse", align_bytes=64)
-        v_s1 = keep.tile([P, LISTS * J], U8, name="v_s1", align_bytes=64)
-        w_s_raw = keep.tile([P, PASSES, R], U8, name="w_s_raw", align_bytes=64)
-        wd_s = keep.tile([P, 1, N], U8, name="wd_s", align_bytes=64)
-        nc.vector.memset(tab_s[:].bitcast(I32), 0)
+        tab_s = keep.tile([P, T], U8, name="tab_s", tag="slot0", align_bytes=64)
+        v_s = keep.tile([P, PASSES, LISTS * J], U8, name="v_s", align_bytes=64)
+        w_s_raw = keep.tile([P, PASSES, R], U8, name="w_s_raw", tag="slot1", align_bytes=64)
+        nc.vector.memset(tab_s[32:64, :].bitcast(I32), 0)
+        nc.vector.memset(tab_s[64:128, :].bitcast(I32), 0)
         nc.gpsimd.memset(w_s_raw[:].bitcast(I32), 0)
-        nc.vector.memset(v_s1[:].bitcast(I32), 0)
-        nc.vector.memset(wd_s[:].bitcast(I32), 0)
+        nc.vector.memset(v_s[:].bitcast(I32), 0)
 
         warm = keep.tile([P, 2], F32, name="warm")
         nc.vector.memset(warm[:, 0:1], 0.0)
         nc.scalar.activation(out=warm[:, 1:2], in_=warm[:, 0:1], func=ACT.Relu)
 
-        nc.sync.dma_start(out=tab_s[16:32, :].bitcast(I32), in_=tab_scales[1].bitcast(I32))
-        for q in range(QUADS):
-            nc.sync.dma_start(
-                out=tab_s[32 * q : 32 * q + 4, :].bitcast(I32),
-                in_=tab_scales[0, 4 * q : 4 * q + 4, :].bitcast(I32),
-            )
+        nc.sync.dma_start(
+            out=tab_s[0:32, :].bitcast(I32), in_=tab_scales.rearrange("a q t -> (a q) t").bitcast(I32)
+        )
+        w_w_raw = keep.tile([P, PASSES, 2 * R], U8, name="w_w_raw", tag="slot2", align_bytes=64)
+        nc.sync.dma_start(out=w_w_raw[:].bitcast(I32), in_=w_words.rearrange("a p n -> p a n").bitcast(I32))
         tab_w = keep.tile([P, T], I32, name="tab_w", align_bytes=64)
         nc.sync.dma_start(out=tab_w[:], in_=tab_words[0].rearrange("p t b -> p (t b)").bitcast(I32))
-        w_w_raw = keep.tile([P, PASSES, 2 * R], U8, name="w_w_raw", align_bytes=64)
-        nc.sync.dma_start(out=w_w_raw[:].bitcast(I32), in_=w_words.rearrange("a p n -> p a n").bitcast(I32))
         load_scale_rows(nc.gpsimd, w_s_raw, w_scales)
 
-        wc_raw = [keep.tile([P, PACK, R], F32, name=f"wc_raw{a}") for a in range(PASSES)]
-
-        def load_rows(raw, src, a):
+        def load_rows(name, tag, src, a):
+            raw = keep.tile([P, PACK, src.shape[1]], F32, name=name, tag=tag, align_bytes=64)
             rows = src[a * P * PACK : (a + 1) * P * PACK, :]
             nc.sync.dma_start(out=raw[:], in_=rows.rearrange("(p i) n -> p i n", i=PACK))
+            return raw
 
+        wc_raw = [load_rows("wc_raw0", "wc_raw0", wc, 0)]
+
+        v_rows = keep.tile([P, LISTS * J], U8, name="v_rows", align_bytes=64)
+        nc.vector.tensor_copy(v_rows[:], tab_s[:].indirect(offsets[:]))
         for a in range(PASSES):
-            load_rows(wc_raw[a], wc, a)
+            for q in range(QUADS):
+                row = 16 * a + 4 * q
+                nc.scalar.dma_start(
+                    out=v_s[32 * q : 32 * q + 4, a, :].bitcast(I32), in_=v_rows[row : row + 4, :].bitcast(I32)
+                )
 
-        v_s0 = keep.tile([P, LISTS * J], U8, name="v_s0", align_bytes=64)
-        nc.vector.tensor_copy(v_s0[:], tab_s[:].indirect(offsets[:]))
-        for q in range(QUADS):
-            nc.scalar.dma_start(
-                out=v_s1[32 * q : 32 * q + 4, :].bitcast(I32),
-                in_=v_s0[16 + 4 * q : 20 + 4 * q, :].bitcast(I32),
-            )
-        v_s = (v_s0, v_s1)
-
-        c_raw = [
-            keep.tile([P, PACK, J], F32, name="c_raw0", tag="reuse", align_bytes=64),
-            keep.tile([P, PACK, J], F32, name="c_raw1"),
+        v_pair = [
+            keep.tile([P, J], U32, name=f"v_pair{g}", tag=f"slot{3 + g}", align_bytes=64) for g in range(LISTS)
         ]
-        for a in range(PASSES):
-            load_rows(c_raw[a], c, a)
-        wd_w = keep.tile([P, N], I32, name="wd_w", align_bytes=64)
-        nc.sync.dma_start(out=wd_w[:], in_=wd_words[0].rearrange("p n b -> p (n b)").bitcast(I32))
-        gate = keep.tile([P, N // P, J], F32, name="gate")
-        nc.sync.dma_start(out=gate[:], in_=gm.rearrange("(u p) j -> p u j", p=P))
-        load_scale_rows(nc.sync, wd_s, wd_scales)
-
-        v_pair = [keep.tile([P, J], U32, name=f"v_pair{g}", align_bytes=64) for g in range(LISTS)]
         v_w = [keep.tile([P, PASSES, 2 * J], U8, name=f"v_w{g}", align_bytes=64) for g in range(LISTS)]
 
         def picks(g):
@@ -127,20 +112,19 @@ def tile_list_pnet_gate_kernel(
             )
 
         def neighbour_sums(g, tag):
-            banks = []
-            for t in range(PACK):
-                bank = psum.tile([P, J], F32, name=f"a{g}_{t}", tag=f"{tag}{t}")
-                for a in range(PASSES):
+            banks = [psum.tile([P, J], F32, name=f"a{g}_{t}", tag=f"{tag}{t}") for t in range(PACK)]
+            for a in range(PASSES):
+                for t in range(PACK):
+                    bank = banks[t]
                     nc.tensor.matmul_mx(
                         out=bank[:],
                         lhsT=w_w[:, a, 2 * P * t : 2 * P * (t + 1)].bitcast(FP4X4),
                         lhsT_scale=w_s[:, a, P * t : P * (t + 1)],
                         rhs=v_w[g][:, a, :].bitcast(FP4X4),
-                        rhs_scale=v_s[a][:, g * J : (g + 1) * J],
+                        rhs_scale=v_s[:, a, g * J : (g + 1) * J],
                         start=(a == 0),
                         stop=(a == PASSES - 1),
                     )
-                banks.append(bank)
             return banks
 
         wc_bf = [keep.tile([P, PACK * R], BF16, name=f"wc_bf{a}", align_bytes=64) for a in range(PASSES)]
@@ -172,7 +156,9 @@ def tile_list_pnet_gate_kernel(
                 in_=c_bf[a][:, PACK * j0 : PACK * j1],
             )
 
+        wc_raw.append(load_rows("wc_raw1", "slot0", wc, 1))
         permute_w()
+        c_raw = [load_rows(f"c_raw{a}", f"slot{1 + a}", c, a) for a in range(PASSES)]
         gather_words(0)
         part_words(0)
         a0 = neighbour_sums(0, "x")
@@ -181,6 +167,13 @@ def tile_list_pnet_gate_kernel(
         a1 = neighbour_sums(1, "y")
         gather_words(2)
         part_words(2)
+        gate = keep.tile([P, N // P, J], F32, name="gate", tag="slot3", align_bytes=64)
+        nc.sync.dma_start(out=gate[:], in_=gm.rearrange("(u p) j -> p u j", p=P))
+        wd_w = keep.tile([P, N], I32, name="wd_w", tag="slot4", align_bytes=64)
+        nc.sync.dma_start(out=wd_w[:], in_=wd_words[0].rearrange("p n b -> p (n b)").bitcast(I32))
+        wd_s = keep.tile([P, 1, N], U8, name="wd_s", tag="slot5", align_bytes=64)
+        nc.vector.memset(wd_s[:].bitcast(I32), 0)
+        load_scale_rows(nc.sync, wd_s, wd_scales)
 
         round_wc(0)
         first = keep.tile([P, PACK, J], F32, name="first")

@@ -47,23 +47,23 @@ def tile_list_pnet_gate_kernel(
         tab_s = keep.tile([P, T], U8, name="tab_s", tag="slot0", align_bytes=64)
         v_s = keep.tile([P, PASSES, LISTS * J], U8, name="v_s", align_bytes=64)
         w_s_raw = keep.tile([P, PASSES, R], U8, name="w_s_raw", tag="slot1", align_bytes=64)
-        nc.vector.memset(tab_s[32:64, :].bitcast(I32), 0)
+        nc.vector.memset(w_s_raw[:].bitcast(I32), 0)
+        load_scale_rows(nc.scalar, w_s_raw, w_scales)
+        nc.gpsimd.memset(tab_s[32:64, :].bitcast(I32), 0)
         nc.vector.memset(tab_s[64:128, :].bitcast(I32), 0)
-        nc.gpsimd.memset(w_s_raw[:].bitcast(I32), 0)
-        nc.vector.memset(v_s[:].bitcast(I32), 0)
+        nc.gpsimd.memset(v_s[:].bitcast(I32), 0)
 
         warm = keep.tile([P, 2], F32, name="warm")
         nc.vector.memset(warm[:, 0:1], 0.0)
         nc.scalar.activation(out=warm[:, 1:2], in_=warm[:, 0:1], func=ACT.Relu)
 
         nc.sync.dma_start(
-            out=tab_s[0:32, :].bitcast(I32), in_=tab_scales.rearrange("a q t -> (a q) t").bitcast(I32)
+            out=tab_s[0:32, :].bitcast(I32), in_=tab_scales.rearrange("a q t -> q a t").bitcast(I32)
         )
-        w_w_raw = keep.tile([P, PASSES, 2 * R], U8, name="w_w_raw", tag="slot2", align_bytes=64)
-        nc.sync.dma_start(out=w_w_raw[:].bitcast(I32), in_=w_words.rearrange("a p n -> p a n").bitcast(I32))
         tab_w = keep.tile([P, T], I32, name="tab_w", align_bytes=64)
         nc.sync.dma_start(out=tab_w[:], in_=tab_words[0].rearrange("p t b -> p (t b)").bitcast(I32))
-        load_scale_rows(nc.gpsimd, w_s_raw, w_scales)
+        w_w_raw = keep.tile([P, PASSES, 2 * R], U8, name="w_w_raw", tag="slot2", align_bytes=64)
+        nc.sync.dma_start(out=w_w_raw[:].bitcast(I32), in_=w_words.rearrange("a p n -> p a n").bitcast(I32))
 
         def load_rows(name, tag, src, a):
             raw = keep.tile([P, PACK, src.shape[1]], F32, name=name, tag=tag, align_bytes=64)
@@ -71,31 +71,25 @@ def tile_list_pnet_gate_kernel(
             nc.sync.dma_start(out=raw[:], in_=rows.rearrange("(p i) n -> p i n", i=PACK))
             return raw
 
-        wc_raw = [load_rows("wc_raw0", "wc_raw0", wc, 0)]
+        wc_raw = [load_rows(f"wc_raw{a}", f"wc_raw{a}", wc, a) for a in range(PASSES)]
 
-        v_rows = keep.tile([P, LISTS * J], U8, name="v_rows", align_bytes=64)
+        v_rows = keep.tile([P, LISTS * J], U8, name="v_rows", tag="slot3", align_bytes=64)
         nc.vector.tensor_copy(v_rows[:], tab_s[:].indirect(offsets[:]))
-        for a in range(PASSES):
-            for q in range(QUADS):
-                row = 16 * a + 4 * q
-                nc.scalar.dma_start(
-                    out=v_s[32 * q : 32 * q + 4, a, :].bitcast(I32), in_=v_rows[row : row + 4, :].bitcast(I32)
-                )
+        for q in range(QUADS):
+            nc.scalar.dma_start(
+                out=v_s[32 * q : 32 * q + 4, :, :].bitcast(I32), in_=v_rows[8 * q : 8 * q + 8, :].bitcast(I32)
+            )
 
-        v_pair = [
-            keep.tile([P, J], U32, name=f"v_pair{g}", tag=f"slot{3 + g}", align_bytes=64) for g in range(LISTS)
-        ]
         v_w = [keep.tile([P, PASSES, 2 * J], U8, name=f"v_w{g}", align_bytes=64) for g in range(LISTS)]
 
         def picks(g):
             return offsets[:, g * J // 16 : (g + 1) * J // 16]
 
-        def gather_words(g):
-            nc.vector.tensor_copy(v_pair[g][:], tab_w[:].bitcast(U32).indirect(picks(g)))
-
-        def part_words(g):
+        def gather_words(g, tag):
+            pair = keep.tile([P, J], U32, name=f"v_pair{g}", tag=tag, align_bytes=64)
+            nc.vector.tensor_copy(pair[:], tab_w[:].bitcast(U32).indirect(picks(g)))
             nc.vector.tensor_copy(
-                v_w[g][:].bitcast(U16), v_pair[g][:].bitcast(U16).rearrange("p (j a) -> p a j", a=PASSES)
+                v_w[g][:].bitcast(U16), pair[:].bitcast(U16).rearrange("p (j a) -> p a j", a=PASSES)
             )
 
         w_w = keep.tile([P, PASSES, 2 * R], U8, name="w_w", align_bytes=64)
@@ -113,8 +107,8 @@ def tile_list_pnet_gate_kernel(
 
         def neighbour_sums(g, tag):
             banks = [psum.tile([P, J], F32, name=f"a{g}_{t}", tag=f"{tag}{t}") for t in range(PACK)]
-            for a in range(PASSES):
-                for t in range(PACK):
+            for t in range(PACK):
+                for a in range(PASSES):
                     bank = banks[t]
                     nc.tensor.matmul_mx(
                         out=bank[:],
@@ -127,18 +121,22 @@ def tile_list_pnet_gate_kernel(
                     )
             return banks
 
-        wc_bf = [keep.tile([P, PACK * R], BF16, name=f"wc_bf{a}", align_bytes=64) for a in range(PASSES)]
+        wc_bf = [
+            keep.tile([P, PACK * R], BF16, name=f"wc_bf{a}", tag=tag, align_bytes=64)
+            for a, tag in enumerate(("slot3", "wc_bf1"))
+        ]
         c_bf = [keep.tile([P, PACK * J], BF16, name=f"c_bf{a}", align_bytes=64) for a in range(PASSES)]
         wc_w = [keep.tile([P, R], U32, name=f"wc_w{a}", align_bytes=64) for a in range(PASSES)]
         wc_s = [keep.tile([P, R], U8, name=f"wc_s{a}", align_bytes=64) for a in range(PASSES)]
         c_w = [keep.tile([P, J], U32, name=f"c_w{a}", align_bytes=64) for a in range(PASSES)]
         c_s = [keep.tile([P, J], U8, name=f"c_s{a}", align_bytes=64) for a in range(PASSES)]
 
-        def round_wc(a):
-            nc.scalar.copy(
-                out=wc_bf[a][:].rearrange("p (t m i) -> p m i t", t=PACK, i=PACK),
-                in_=wc_raw[a][:].rearrange("p i (m t) -> p m i t", t=PACK),
-            )
+        def round_wc(copy, a):
+            for t in range(0, PACK, 2):
+                copy(
+                    out=wc_bf[a][:].rearrange("p (t m i) -> p m i t", t=PACK, i=PACK)[:, :, :, t : t + 2],
+                    in_=wc_raw[a][:].rearrange("p i (m t) -> p m i t", t=PACK)[:, :, :, t : t + 2],
+                )
 
         def round_c(a, j0, j1):
             nc.scalar.copy(
@@ -156,48 +154,33 @@ def tile_list_pnet_gate_kernel(
                 in_=c_bf[a][:, PACK * j0 : PACK * j1],
             )
 
-        wc_raw.append(load_rows("wc_raw1", "slot0", wc, 1))
         permute_w()
-        c_raw = [load_rows(f"c_raw{a}", f"slot{1 + a}", c, a) for a in range(PASSES)]
-        gather_words(0)
-        part_words(0)
+        c_raw = [load_rows(f"c_raw{a}", f"slot{a}", c, a) for a in range(PASSES)]
+        gather_words(0, "slot4")
         a0 = neighbour_sums(0, "x")
-        gather_words(1)
-        part_words(1)
+        gather_words(1, "slot2")
         a1 = neighbour_sums(1, "y")
-        gather_words(2)
-        part_words(2)
-        gate = keep.tile([P, N // P, J], F32, name="gate", tag="slot3", align_bytes=64)
+        gather_words(2, "slot4")
+        gate = keep.tile([P, N // P, J], F32, name="gate", tag="slot4", align_bytes=64)
         nc.sync.dma_start(out=gate[:], in_=gm.rearrange("(u p) j -> p u j", p=P))
-        wd_w = keep.tile([P, N], I32, name="wd_w", tag="slot4", align_bytes=64)
-        nc.sync.dma_start(out=wd_w[:], in_=wd_words[0].rearrange("p n b -> p (n b)").bitcast(I32))
-        wd_s = keep.tile([P, 1, N], U8, name="wd_s", tag="slot5", align_bytes=64)
-        nc.vector.memset(wd_s[:].bitcast(I32), 0)
+        wd_s = keep.tile([P, 1, N], U8, name="wd_s", tag="slot2", align_bytes=64)
+        nc.gpsimd.memset(wd_s[:].bitcast(I32), 0)
         load_scale_rows(nc.sync, wd_s, wd_scales)
 
-        round_wc(0)
+        round_wc(nc.scalar.copy, 0)
         first = keep.tile([P, PACK, J], F32, name="first")
         for t in range(PACK):
             nc.scalar.copy(out=first[:, t, :], in_=a0[t][:])
         a2 = neighbour_sums(2, "x")
-        round_wc(1)
+        round_wc(nc.vector.tensor_copy, 1)
         quantize_wc(0)
+        wd_w = keep.tile([P, N], I32, name="wd_w", tag="slot3", align_bytes=64)
+        nc.sync.dma_start(out=wd_w[:], in_=wd_words[0].rearrange("p n b -> p (n b)").bitcast(I32))
         second = keep.tile([P, PACK, J], F32, name="second")
         for t in range(PACK):
             nc.vector.tensor_tensor(second[:, t, :], a1[t][:], first[:, t, :], ALU.max)
-        for j0 in range(0, J, 256):
-            nc.gpsimd.tensor_scalar(
-                c_bf[0][:, PACK * j0 : PACK * (j0 + 256)].rearrange("p (j i) -> p j i", i=PACK),
-                c_raw[0][:, :, j0 : j0 + 256].rearrange("p i j -> p j i"),
-                1.0,
-                0.0,
-                ALU.mult,
-                ALU.add,
-            )
+        round_c(0, 0, J)
         quantize_wc(1)
-        pooled = keep.tile([P, PACK, J], F32, name="pooled")
-        for t in range(PACK):
-            nc.vector.tensor_tensor(pooled[:, t, :], a2[t][:], second[:, t, :], ALU.max)
         quantize_c(0, 0, J)
 
         own = []
@@ -219,6 +202,9 @@ def tile_list_pnet_gate_kernel(
                     )
             own.append(bank)
 
+        pooled = keep.tile([P, PACK, J], F32, name="pooled")
+        for t in range(PACK):
+            nc.vector.tensor_tensor(pooled[:, t, :], a2[t][:], second[:, t, :], ALU.max)
         out_rows = out.rearrange("(u p) j -> p u j", p=P)
         for q in range(PARTS):
             j0, j1 = q * JQ, (q + 1) * JQ

@@ -23,14 +23,10 @@ PASSES = K // (P * PACK)
 QUADS = 4
 JQ = 128
 PARTS = J // JQ
-
-
-def load_scale_rows(queue, plane, scales):
-    for q in range(QUADS):
-        queue.dma_start(
-            out=plane[32 * q : 32 * q + 4, :, :].bitcast(I32),
-            in_=scales[:, 4 * q : 4 * q + 4, :].rearrange("a r n -> r a n").bitcast(I32),
-        )
+ROWS = slice(96, 128)
+W_COL = J
+WD_COL = W_COL + R
+PLANE = WD_COL + N
 
 
 def tile_list_pnet_gate_kernel(
@@ -45,20 +41,24 @@ def tile_list_pnet_gate_kernel(
         nc.sync.dma_start(offsets[:], offs)
 
         tab_s = keep.tile([P, T], U8, name="tab_s", tag="slot0", align_bytes=64)
-        v_s = keep.tile([P, PASSES, LISTS * J], U8, name="v_s", align_bytes=64)
-        w_s_raw = keep.tile([P, PASSES, R], U8, name="w_s_raw", tag="slot1", align_bytes=64)
-        nc.vector.memset(w_s_raw[:].bitcast(I32), 0)
-        load_scale_rows(nc.scalar, w_s_raw, w_scales)
-        nc.gpsimd.memset(tab_s[32:64, :].bitcast(I32), 0)
-        nc.vector.memset(tab_s[64:128, :].bitcast(I32), 0)
-        nc.gpsimd.memset(v_s[:].bitcast(I32), 0)
+        planes = keep.tile([P, PASSES, PLANE], U8, name="planes", align_bytes=64)
+        planes_late = keep.tile([P, PASSES, 2 * J], U8, name="planes_late", align_bytes=64)
+        rows_s = keep.tile([P, PLANE], U8, name="rows_s", tag="slot3", align_bytes=64)
+        w_s_raw = keep.tile([P, R], U8, name="w_s_raw", align_bytes=64)
+        nc.vector.memset(tab_s[0:96, :].bitcast(I32), 0)
+        nc.vector.memset(w_s_raw[0:96, :].bitcast(I32), 0)
+        nc.vector.memset(planes[:].bitcast(I32), 0)
+        nc.vector.memset(planes_late[:].bitcast(I32), 0)
 
         warm = keep.tile([P, 2], F32, name="warm")
         nc.vector.memset(warm[:, 0:1], 0.0)
         nc.scalar.activation(out=warm[:, 1:2], in_=warm[:, 0:1], func=ACT.Relu)
 
+        nc.sync.dma_start(out=tab_s[ROWS, :].bitcast(I32), in_=tab_scales.rearrange("a q t -> q a t").bitcast(I32))
+        nc.sync.dma_start(out=w_s_raw[ROWS, :].bitcast(I32), in_=w_scales.rearrange("a q r -> q a r").bitcast(I32))
         nc.sync.dma_start(
-            out=tab_s[0:32, :].bitcast(I32), in_=tab_scales.rearrange("a q t -> q a t").bitcast(I32)
+            out=rows_s[ROWS, WD_COL:PLANE].bitcast(I32),
+            in_=wd_scales.rearrange("a q n -> q a n").bitcast(I32).broadcast_to([16, PASSES, N // 4]),
         )
         tab_w = keep.tile([P, T], I32, name="tab_w", align_bytes=64)
         nc.sync.dma_start(out=tab_w[:], in_=tab_words[0].rearrange("p t b -> p (t b)").bitcast(I32))
@@ -71,35 +71,44 @@ def tile_list_pnet_gate_kernel(
             nc.sync.dma_start(out=raw[:], in_=rows.rearrange("(p i) n -> p i n", i=PACK))
             return raw
 
-        wc_raw = [load_rows(f"wc_raw{a}", f"wc_raw{a}", wc, a) for a in range(PASSES)]
+        wc_raw = [load_rows("wc_raw0", "wc_raw0", wc, 0)]
 
-        v_rows = keep.tile([P, LISTS * J], U8, name="v_rows", tag="slot3", align_bytes=64)
-        nc.vector.tensor_copy(v_rows[:], tab_s[:].indirect(offsets[:]))
-        for q in range(QUADS):
-            nc.scalar.dma_start(
-                out=v_s[32 * q : 32 * q + 4, :, :].bitcast(I32), in_=v_rows[8 * q : 8 * q + 8, :].bitcast(I32)
-            )
+        def spread_rows(queue, dst, rows):
+            for q in range(QUADS):
+                queue.dma_start(
+                    out=dst[32 * q : 32 * q + 4, :, :].bitcast(I32),
+                    in_=rows[96 + 8 * q : 96 + 8 * q + 8, :].bitcast(I32),
+                )
+
+        first_picks = offsets[:, 0 : J // 16]
+        late_picks = offsets[:, J // 16 : LISTS * J // 16]
+        v_rows = keep.tile([P, J], U8, name="v_rows", tag="slot6", align_bytes=64)
+        nc.vector.tensor_copy(v_rows[:], tab_s[:].indirect(first_picks))
+        nc.vector.tensor_copy(
+            rows_s[:, W_COL:WD_COL].rearrange("p (t m) -> p t m", t=PACK),
+            w_s_raw[:].rearrange("p (m t) -> p t m", t=PACK),
+        )
+        nc.vector.tensor_copy(rows_s[ROWS, 0:W_COL].bitcast(I32), v_rows[ROWS, :].bitcast(I32))
+        spread_rows(nc.scalar, planes, rows_s)
+        v_rows_late = keep.tile([P, 2 * J], U8, name="v_rows_late", tag="slot6", align_bytes=64)
+        nc.vector.tensor_copy(v_rows_late[:], tab_s[:].indirect(late_picks))
+        spread_rows(nc.scalar, planes_late, v_rows_late)
+        wc_raw.append(load_rows("wc_raw1", "slot0", wc, 1))
 
         v_w = [keep.tile([P, PASSES, 2 * J], U8, name=f"v_w{g}", align_bytes=64) for g in range(LISTS)]
+        v_planes = (planes[:, :, 0:J], planes_late[:, :, 0:J], planes_late[:, :, J : 2 * J])
 
-        def picks(g):
-            return offsets[:, g * J // 16 : (g + 1) * J // 16]
-
-        def gather_words(g, tag):
-            pair = keep.tile([P, J], U32, name=f"v_pair{g}", tag=tag, align_bytes=64)
-            nc.vector.tensor_copy(pair[:], tab_w[:].bitcast(U32).indirect(picks(g)))
-            nc.vector.tensor_copy(
-                v_w[g][:].bitcast(U16), pair[:].bitcast(U16).rearrange("p (j a) -> p a j", a=PASSES)
-            )
+        def gather_words(name, picks, lists):
+            pair = keep.tile([P, len(lists), J], U32, name=name, tag="slot4", align_bytes=64)
+            nc.vector.tensor_copy(pair[:].rearrange("p g j -> p (g j)"), tab_w[:].bitcast(U32).indirect(picks))
+            for n, g in enumerate(lists):
+                nc.vector.tensor_copy(
+                    v_w[g][:].bitcast(U16), pair[:, n, :].bitcast(U16).rearrange("p (j a) -> p a j", a=PASSES)
+                )
 
         w_w = keep.tile([P, PASSES, 2 * R], U8, name="w_w", align_bytes=64)
-        w_s = keep.tile([P, PASSES, R], U8, name="w_s", align_bytes=64)
 
         def permute_w():
-            nc.vector.tensor_copy(
-                w_s[:].rearrange("p a (t m) -> p a t m", t=PACK),
-                w_s_raw[:].rearrange("p a (m t) -> p a t m", t=PACK),
-            )
             nc.vector.tensor_copy(
                 w_w[:].bitcast(U16).rearrange("p a (t m) -> p a t m", t=PACK),
                 w_w_raw[:].bitcast(U16).rearrange("p a (m t) -> p a t m", t=PACK),
@@ -113,81 +122,80 @@ def tile_list_pnet_gate_kernel(
                     nc.tensor.matmul_mx(
                         out=bank[:],
                         lhsT=w_w[:, a, 2 * P * t : 2 * P * (t + 1)].bitcast(FP4X4),
-                        lhsT_scale=w_s[:, a, P * t : P * (t + 1)],
+                        lhsT_scale=planes[:, a, W_COL + P * t : W_COL + P * (t + 1)],
                         rhs=v_w[g][:, a, :].bitcast(FP4X4),
-                        rhs_scale=v_s[:, a, g * J : (g + 1) * J],
+                        rhs_scale=v_planes[g][:, a, :],
                         start=(a == 0),
                         stop=(a == PASSES - 1),
                     )
             return banks
 
-        wc_bf = [
-            keep.tile([P, PACK * R], BF16, name=f"wc_bf{a}", tag=tag, align_bytes=64)
-            for a, tag in enumerate(("slot3", "wc_bf1"))
-        ]
-        c_bf = [keep.tile([P, PACK * J], BF16, name=f"c_bf{a}", align_bytes=64) for a in range(PASSES)]
+        wc_bf, c_bf, c_w = {}, {}, {}
         wc_w = [keep.tile([P, R], U32, name=f"wc_w{a}", align_bytes=64) for a in range(PASSES)]
         wc_s = [keep.tile([P, R], U8, name=f"wc_s{a}", align_bytes=64) for a in range(PASSES)]
-        c_w = [keep.tile([P, J], U32, name=f"c_w{a}", align_bytes=64) for a in range(PASSES)]
         c_s = [keep.tile([P, J], U8, name=f"c_s{a}", align_bytes=64) for a in range(PASSES)]
 
-        def round_wc(copy, a):
-            for t in range(0, PACK, 2):
-                copy(
-                    out=wc_bf[a][:].rearrange("p (t m i) -> p m i t", t=PACK, i=PACK)[:, :, :, t : t + 2],
-                    in_=wc_raw[a][:].rearrange("p i (m t) -> p m i t", t=PACK)[:, :, :, t : t + 2],
-                )
-
-        def round_c(a, j0, j1):
+        def round_wc(a, tag):
+            wc_bf[a] = keep.tile([P, PACK * R], BF16, name=f"wc_bf{a}", tag=tag, align_bytes=64)
             nc.scalar.copy(
-                out=c_bf[a][:, PACK * j0 : PACK * j1].rearrange("p (b e i) -> p b i e", e=4, i=PACK),
+                out=wc_bf[a][:].rearrange("p (t m i) -> p m i t", t=PACK, i=PACK),
+                in_=wc_raw[a][:].rearrange("p i (m t) -> p m i t", t=PACK),
+            )
+
+        def round_c(dst, a, j0, j1):
+            nc.scalar.copy(
+                out=dst[:].rearrange("p (b e i) -> p b i e", e=4, i=PACK),
                 in_=c_raw[a][:, :, j0:j1].rearrange("p i (b e) -> p b i e", e=4),
             )
 
         def quantize_wc(a):
             nc.vector.quantize_mx(out=wc_w[a][:].bitcast(FP8X4), scales=wc_s[a][:], in_=wc_bf[a][:])
 
-        def quantize_c(a, j0, j1):
-            nc.vector.quantize_mx(
-                out=c_w[a][:, j0:j1].bitcast(FP8X4),
-                scales=c_s[a][:, j0:j1],
-                in_=c_bf[a][:, PACK * j0 : PACK * j1],
-            )
+        def quantize_c(src, a, j0, j1):
+            nc.vector.quantize_mx(out=c_w[a][:, j0:j1].bitcast(FP8X4), scales=c_s[a][:, j0:j1], in_=src[:])
 
         permute_w()
-        c_raw = [load_rows(f"c_raw{a}", f"slot{a}", c, a) for a in range(PASSES)]
-        gather_words(0, "slot4")
+        c_raw = [load_rows(f"c_raw{a}", tag, c, a) for a, tag in enumerate(("slot2", "slot3"))]
+        gather_words("v_pair", first_picks, (0,))
         a0 = neighbour_sums(0, "x")
-        gather_words(1, "slot2")
+        gather_words("v_pair_late", late_picks, (1, 2))
         a1 = neighbour_sums(1, "y")
-        gather_words(2, "slot4")
-        gate = keep.tile([P, N // P, J], F32, name="gate", tag="slot4", align_bytes=64)
-        nc.sync.dma_start(out=gate[:], in_=gm.rearrange("(u p) j -> p u j", p=P))
-        wd_s = keep.tile([P, 1, N], U8, name="wd_s", tag="slot2", align_bytes=64)
-        nc.gpsimd.memset(wd_s[:].bitcast(I32), 0)
-        load_scale_rows(nc.sync, wd_s, wd_scales)
 
-        round_wc(nc.scalar.copy, 0)
-        first = keep.tile([P, PACK, J], F32, name="first")
+        round_wc(0, "wc_bf0")
+        first = keep.tile([P, PACK, J], F32, name="first", tag="slot5", align_bytes=64)
         for t in range(PACK):
             nc.scalar.copy(out=first[:, t, :], in_=a0[t][:])
         a2 = neighbour_sums(2, "x")
-        round_wc(nc.vector.tensor_copy, 1)
+        round_wc(1, "slot4")
         quantize_wc(0)
-        wd_w = keep.tile([P, N], I32, name="wd_w", tag="slot3", align_bytes=64)
-        nc.sync.dma_start(out=wd_w[:], in_=wd_words[0].rearrange("p n b -> p (n b)").bitcast(I32))
         second = keep.tile([P, PACK, J], F32, name="second")
         for t in range(PACK):
             nc.vector.tensor_tensor(second[:, t, :], a1[t][:], first[:, t, :], ALU.max)
-        round_c(0, 0, J)
+        c_bf[0] = keep.tile([P, PACK * J], BF16, name="c_bf0", align_bytes=64)
+        for j0 in range(0, J, 256):
+            nc.gpsimd.tensor_scalar(
+                c_bf[0][:, PACK * j0 : PACK * (j0 + 256)].rearrange("p (j i) -> p j i", i=PACK),
+                c_raw[0][:, :, j0 : j0 + 256].rearrange("p i j -> p j i"),
+                1.0,
+                0.0,
+                ALU.mult,
+                ALU.add,
+            )
         quantize_wc(1)
-        quantize_c(0, 0, J)
+        wd_w = keep.tile([P, N], I32, name="wd_w", tag="slot4", align_bytes=64)
+        nc.sync.dma_start(out=wd_w[:], in_=wd_words[0].rearrange("p n b -> p (n b)").bitcast(I32))
+        gate = keep.tile([P, N // P, J], F32, name="gate", tag="slot2", align_bytes=64)
+        nc.sync.dma_start(out=gate[:], in_=gm.rearrange("(u p) j -> p u j", p=P))
+        c_w[0] = keep.tile([P, J], U32, name="c_w0", tag="slot5", align_bytes=64)
+        quantize_c(c_bf[0], 0, 0, J)
+        c_w[1] = keep.tile([P, J], U32, name="c_w1", align_bytes=64)
 
         own = []
         for q in range(PARTS):
             j0, j1 = q * JQ, (q + 1) * JQ
-            round_c(1, j0, j1)
-            quantize_c(1, j0, j1)
+            c_part = keep.tile([P, PACK * JQ], BF16, name=f"c_part{q}", tag=("slot0", "slot8", "c2", "c3")[q], align_bytes=64)
+            round_c(c_part, 1, j0, j1)
+            quantize_c(c_part, 1, j0, j1)
             bank = psum.tile([P, PACK, JQ], F32, name=f"own{q}", tag=f"y{q}")
             for t in range(PACK):
                 for a in range(PASSES):
@@ -224,7 +232,7 @@ def tile_list_pnet_gate_kernel(
                 nc.tensor.matmul_mx(
                     out=bank[:, u, :],
                     lhsT=wd_w[:, P * u : P * (u + 1)].bitcast(FP8X4),
-                    lhsT_scale=wd_s[:, 0, P * u : P * (u + 1)],
+                    lhsT_scale=planes[:, 0, WD_COL + P * u : WD_COL + P * (u + 1)],
                     rhs=h_w[:].bitcast(FP8X4),
                     rhs_scale=h_s[:],
                     start=True,

@@ -60,10 +60,10 @@ def tile_list_pnet_gate_kernel(
             out=rows_s[ROWS, WD_COL:PLANE].bitcast(I32),
             in_=wd_scales.rearrange("a q n -> q a n").bitcast(I32).broadcast_to([16, PASSES, N // 4]),
         )
-        tab_w = keep.tile([P, T], I32, name="tab_w", align_bytes=64)
-        nc.sync.dma_start(out=tab_w[:], in_=tab_words[0].rearrange("p t b -> p (t b)").bitcast(I32))
         w_w_raw = keep.tile([P, PASSES, 2 * R], U8, name="w_w_raw", tag="slot2", align_bytes=64)
         nc.sync.dma_start(out=w_w_raw[:].bitcast(I32), in_=w_words.rearrange("a p n -> p a n").bitcast(I32))
+        tab_w = keep.tile([P, T], I32, name="tab_w", align_bytes=64)
+        nc.sync.dma_start(out=tab_w[:], in_=tab_words[0].rearrange("p t b -> p (t b)").bitcast(I32))
 
         def load_rows(name, tag, src, a):
             raw = keep.tile([P, PACK, src.shape[1]], F32, name=name, tag=tag, align_bytes=64)

@@ -1,6 +1,7 @@
 from contextlib import ExitStack
 
 import concourse.mybir as mybir
+from concourse.masks import make_identity
 
 K, R, N, T, J = 1024, 512, 256, 4096, 512
 LISTS = 3
@@ -21,12 +22,14 @@ P = 128
 PACK = 4
 PASSES = K // (P * PACK)
 QUADS = 4
-JQ = 128
-PARTS = J // JQ
+PARTS = J // P
 ROWS = slice(96, 128)
-W_COL = J
+EARLY = 2
+W_COL = EARLY * J
 WD_COL = W_COL + R
-PLANE = WD_COL + N
+PLANE = WD_COL + P
+RAW = PACK * J * 4
+BY_TENSOR = 0
 
 
 def tile_list_pnet_gate_kernel(
@@ -35,6 +38,7 @@ def tile_list_pnet_gate_kernel(
     nc = tc.nc
     with ExitStack() as ctx:
         keep = ctx.enter_context(tc.tile_pool(name="keep", bufs=1))
+        relay = ctx.enter_context(tc.tile_pool(name="relay", bufs=1))
         psum = ctx.enter_context(tc.psum_pool(name="psum", bufs=1))
 
         offsets = keep.tile([P, LISTS * J // 16], U16, name="offsets")
@@ -42,202 +46,208 @@ def tile_list_pnet_gate_kernel(
 
         tab_s = keep.tile([P, T], U8, name="tab_s", tag="slot0", align_bytes=64)
         planes = keep.tile([P, PASSES, PLANE], U8, name="planes", align_bytes=64)
-        planes_late = keep.tile([P, PASSES, 2 * J], U8, name="planes_late", align_bytes=64)
+        planes_late = keep.tile([P, PASSES, J], U8, name="planes_late", align_bytes=64)
         rows_s = keep.tile([P, PLANE], U8, name="rows_s", tag="slot3", align_bytes=64)
-        w_s_raw = keep.tile([P, R], U8, name="w_s_raw", align_bytes=64)
+        identity = keep.tile([P, P], F32, name="identity")
         nc.vector.memset(tab_s[0:96, :].bitcast(I32), 0)
-        nc.vector.memset(w_s_raw[0:96, :].bitcast(I32), 0)
-        nc.vector.memset(planes[:].bitcast(I32), 0)
-        nc.vector.memset(planes_late[:].bitcast(I32), 0)
+        nc.gpsimd.memset(planes[:].bitcast(I32), 0)
+        nc.gpsimd.memset(planes_late[:].bitcast(I32), 0)
+        make_identity(nc, identity[:])
+
+        nc.scalar.dma_start(out=tab_s[ROWS, :].bitcast(I32), in_=tab_scales.rearrange("a q t -> q a t").bitcast(I32))
+        nc.sync.dma_start(
+            out=rows_s[ROWS, W_COL:WD_COL].bitcast(I32), in_=w_scales.rearrange("a q r -> q a r").bitcast(I32)
+        )
+        nc.scalar.dma_start(
+            out=rows_s[ROWS, WD_COL:PLANE].bitcast(I32),
+            in_=wd_scales[0].rearrange("q (u n) -> (q u) n", n=P).bitcast(I32),
+        )
+        tab_w = keep.tile([P, T], I32, name="tab_w", tag="slot7", align_bytes=64)
+        nc.sync.dma_start(out=tab_w[:], in_=tab_words[0].rearrange("p t b -> p (t b)").bitcast(I32))
+        w_w = keep.tile([P, PASSES, 2 * R], U8, name="w_w", align_bytes=64)
+        nc.sync.dma_start(out=w_w[:].bitcast(I32), in_=w_words.rearrange("a p n -> p a n").bitcast(I32))
 
         warm = keep.tile([P, 2], F32, name="warm")
         nc.vector.memset(warm[:, 0:1], 0.0)
         nc.scalar.activation(out=warm[:, 1:2], in_=warm[:, 0:1], func=ACT.Relu)
 
-        nc.sync.dma_start(out=tab_s[ROWS, :].bitcast(I32), in_=tab_scales.rearrange("a q t -> q a t").bitcast(I32))
-        nc.sync.dma_start(out=w_s_raw[ROWS, :].bitcast(I32), in_=w_scales.rearrange("a q r -> q a r").bitcast(I32))
-        nc.sync.dma_start(
-            out=rows_s[ROWS, WD_COL:PLANE].bitcast(I32),
-            in_=wd_scales.rearrange("a q n -> q a n").bitcast(I32).broadcast_to([16, PASSES, N // 4]),
-        )
-        w_w_raw = keep.tile([P, PASSES, 2 * R], U8, name="w_w_raw", tag="slot2", align_bytes=64)
-        nc.sync.dma_start(out=w_w_raw[:].bitcast(I32), in_=w_words.rearrange("a p n -> p a n").bitcast(I32))
-        tab_w = keep.tile([P, T], I32, name="tab_w", align_bytes=64)
-        nc.sync.dma_start(out=tab_w[:], in_=tab_words[0].rearrange("p t b -> p (t b)").bitcast(I32))
-
-        def load_rows(name, tag, src, a):
-            raw = keep.tile([P, PACK, src.shape[1]], F32, name=name, tag=tag, align_bytes=64)
+        def load_rows(raw, src, a):
             rows = src[a * P * PACK : (a + 1) * P * PACK, :]
             nc.sync.dma_start(out=raw[:], in_=rows.rearrange("(p i) n -> p i n", i=PACK))
             return raw
 
-        wc_raw = [load_rows("wc_raw0", "wc_raw0", wc, 0)]
-
-        def spread_rows(queue, dst, rows):
+        def spread_rows(dst, rows):
             for q in range(QUADS):
-                queue.dma_start(
+                nc.sync.dma_start(
                     out=dst[32 * q : 32 * q + 4, :, :].bitcast(I32),
                     in_=rows[96 + 8 * q : 96 + 8 * q + 8, :].bitcast(I32),
                 )
 
-        first_picks = offsets[:, 0 : J // 16]
-        late_picks = offsets[:, J // 16 : LISTS * J // 16]
-        v_rows = keep.tile([P, J], U8, name="v_rows", tag="slot6", align_bytes=64)
-        nc.vector.tensor_copy(v_rows[:], tab_s[:].indirect(first_picks))
-        nc.vector.tensor_copy(
-            rows_s[:, W_COL:WD_COL].rearrange("p (t m) -> p t m", t=PACK),
-            w_s_raw[:].rearrange("p (m t) -> p t m", t=PACK),
-        )
+        v_rows = relay.tile([P, W_COL], U8, name="v_rows", offset=RAW - J)
+        nc.vector.tensor_copy(v_rows[:], tab_s[:].indirect(offsets[:, 0 : W_COL // 16]))
         nc.vector.tensor_copy(rows_s[ROWS, 0:W_COL].bitcast(I32), v_rows[ROWS, :].bitcast(I32))
-        spread_rows(nc.scalar, planes, rows_s)
-        v_rows_late = keep.tile([P, 2 * J], U8, name="v_rows_late", tag="slot6", align_bytes=64)
-        nc.vector.tensor_copy(v_rows_late[:], tab_s[:].indirect(late_picks))
-        spread_rows(nc.scalar, planes_late, v_rows_late)
-        wc_raw.append(load_rows("wc_raw1", "slot0", wc, 1))
+        spread_rows(planes, rows_s)
+        wc_raw = [load_rows(relay.tile([P, PACK, R], F32, name="wc_raw0", offset=RAW), wc, 0)]
+        v_rows_late = relay.tile([P, J], U8, name="v_rows_late", offset=RAW - J)
+        nc.vector.tensor_copy(v_rows_late[:], tab_s[:].indirect(offsets[:, W_COL // 16 :]))
+        spread_rows(planes_late, v_rows_late)
+        c_raw = [load_rows(keep.tile([P, PACK, J], F32, name="c_raw0", tag="slot0", align_bytes=64), c, 0)]
+        wc_raw.append(load_rows(keep.tile([P, PACK, R], F32, name="wc_raw1", tag="slot3", align_bytes=64), wc, 1))
+        c_raw.append(load_rows(relay.tile([P, PACK, J], F32, name="c_raw1", offset=0), c, 1))
 
-        v_w = [keep.tile([P, PASSES, 2 * J], U8, name=f"v_w{g}", align_bytes=64) for g in range(LISTS)]
-        v_planes = (planes[:, :, 0:J], planes_late[:, :, 0:J], planes_late[:, :, J : 2 * J])
+        v_planes = (planes[:, :, 0:J], planes[:, :, J : 2 * J], planes_late[:])
+        first_pair = keep.tile([P, J], U32, name="first_pair", tag="slot2", align_bytes=64)
+        nc.vector.tensor_copy(first_pair[:], tab_w[:].bitcast(U32).indirect(offsets[:, 0 : J // 16]))
+        v_first = []
+        for a in range(PASSES):
+            v_first.append(keep.tile([P, 2 * J], U8, name=f"v_first{a}", align_bytes=64))
+            nc.vector.tensor_copy(v_first[a][:].bitcast(U16), first_pair[:].bitcast(U16)[:, a :: PASSES])
+        v_w = [[v_first[a][:] for a in range(PASSES)]]
 
-        def gather_words(name, picks, lists):
-            pair = keep.tile([P, len(lists), J], U32, name=name, tag="slot4", align_bytes=64)
-            nc.vector.tensor_copy(pair[:].rearrange("p g j -> p (g j)"), tab_w[:].bitcast(U32).indirect(picks))
-            for n, g in enumerate(lists):
-                nc.vector.tensor_copy(
-                    v_w[g][:].bitcast(U16), pair[:, n, :].bitcast(U16).rearrange("p (j a) -> p a j", a=PASSES)
-                )
-
-        w_w = keep.tile([P, PASSES, 2 * R], U8, name="w_w", align_bytes=64)
-
-        def permute_w():
+        late_pair = keep.tile([P, LISTS - 1, J], U32, name="late_pair", tag="slot2", align_bytes=64)
+        nc.vector.tensor_copy(
+            late_pair[:].rearrange("p g j -> p (g j)"), tab_w[:].bitcast(U32).indirect(offsets[:, J // 16 :])
+        )
+        for g in range(1, LISTS):
+            parted = keep.tile([P, PASSES, 2 * J], U8, name=f"v_late{g}", align_bytes=64)
             nc.vector.tensor_copy(
-                w_w[:].bitcast(U16).rearrange("p a (t m) -> p a t m", t=PACK),
-                w_w_raw[:].bitcast(U16).rearrange("p a (m t) -> p a t m", t=PACK),
+                parted[:].bitcast(U16), late_pair[:, g - 1, :].bitcast(U16).rearrange("p (j a) -> p a j", a=PASSES)
             )
+            v_w.append([parted[:, a, :] for a in range(PASSES)])
 
-        def neighbour_sums(g, tag):
-            banks = [psum.tile([P, J], F32, name=f"a{g}_{t}", tag=f"{tag}{t}") for t in range(PACK)]
-            for t in range(PACK):
-                for a in range(PASSES):
-                    bank = banks[t]
-                    nc.tensor.matmul_mx(
-                        out=bank[:],
-                        lhsT=w_w[:, a, 2 * P * t : 2 * P * (t + 1)].bitcast(FP4X4),
-                        lhsT_scale=planes[:, a, W_COL + P * t : W_COL + P * (t + 1)],
-                        rhs=v_w[g][:, a, :].bitcast(FP4X4),
-                        rhs_scale=v_planes[g][:, a, :],
-                        start=(a == 0),
-                        stop=(a == PASSES - 1),
-                    )
+        def neighbour_sums(g, tag, order):
+            banks = [psum.tile([P, R], F32, name=f"a{g}_{q}", tag=f"{tag}{q}") for q in range(PARTS)]
+            for q, a in order:
+                nc.tensor.matmul_mx(
+                    out=banks[q][:],
+                    lhsT=v_w[g][a][:, 2 * P * q : 2 * P * (q + 1)].bitcast(FP4X4),
+                    lhsT_scale=v_planes[g][:, a, P * q : P * (q + 1)],
+                    rhs=w_w[:, a, :].bitcast(FP4X4),
+                    rhs_scale=planes[:, a, W_COL:WD_COL],
+                    start=(a == 0),
+                    stop=(a == PASSES - 1),
+                )
             return banks
 
-        wc_bf, c_bf, c_w = {}, {}, {}
-        wc_w = [keep.tile([P, R], U32, name=f"wc_w{a}", align_bytes=64) for a in range(PASSES)]
+        def dealt(bank):
+            return bank[:].rearrange("p (m t) -> p t m", t=PACK)
+
+        by_pass = [(q, a) for a in range(PASSES) for q in range(PARTS)]
+        by_bank = [(q, a) for q in range(PARTS) for a in range(PASSES)]
+        a0 = neighbour_sums(0, "x", by_pass)
+        a1 = neighbour_sums(1, "y", by_bank)
+
+        wc_w = [
+            keep.tile([P, R], U32, name="wc_w0", align_bytes=64),
+            keep.tile([P, R], U32, name="wc_w1", align_bytes=64),
+        ]
         wc_s = [keep.tile([P, R], U8, name=f"wc_s{a}", align_bytes=64) for a in range(PASSES)]
+        c_w = [keep.tile([P, J], U32, name=f"c_w{a}", align_bytes=64) for a in range(PASSES)]
         c_s = [keep.tile([P, J], U8, name=f"c_s{a}", align_bytes=64) for a in range(PASSES)]
 
-        def round_wc(a, tag):
-            wc_bf[a] = keep.tile([P, PACK * R], BF16, name=f"wc_bf{a}", tag=tag, align_bytes=64)
+        wc_bf = [keep.tile([P, PACK * R], BF16, name=f"wc_bf{a}", align_bytes=64)[:] for a in range(PASSES)]
+        c_parts = [keep.tile([P, PACK * P], BF16, name=f"c_part{q}", align_bytes=64)[:] for q in range(PARTS)]
+
+        def round_scalar(dst, raw):
             nc.scalar.copy(
-                out=wc_bf[a][:].rearrange("p (t m i) -> p m i t", t=PACK, i=PACK),
-                in_=wc_raw[a][:].rearrange("p i (m t) -> p m i t", t=PACK),
+                out=dst.rearrange("p (b e i) -> p b i e", e=4, i=PACK),
+                in_=raw.rearrange("p i (b e) -> p b i e", e=4),
             )
 
-        def round_c(dst, a, j0, j1):
-            nc.scalar.copy(
-                out=dst[:].rearrange("p (b e i) -> p b i e", e=4, i=PACK),
-                in_=c_raw[a][:, :, j0:j1].rearrange("p i (b e) -> p b i e", e=4),
+        def round_gpsimd(dst, raw):
+            nc.gpsimd.tensor_scalar(
+                dst.rearrange("p (j i) -> p j i", i=PACK), raw.rearrange("p i j -> p j i"), 1.0, 0.0, ALU.mult, ALU.add
             )
 
         def quantize_wc(a):
-            nc.vector.quantize_mx(out=wc_w[a][:].bitcast(FP8X4), scales=wc_s[a][:], in_=wc_bf[a][:])
+            nc.vector.quantize_mx(out=wc_w[a][:].bitcast(FP8X4), scales=wc_s[a][:], in_=wc_bf[a])
 
         def quantize_c(src, a, j0, j1):
-            nc.vector.quantize_mx(out=c_w[a][:, j0:j1].bitcast(FP8X4), scales=c_s[a][:, j0:j1], in_=src[:])
+            nc.vector.quantize_mx(out=c_w[a][:, j0:j1].bitcast(FP8X4), scales=c_s[a][:, j0:j1], in_=src)
 
-        permute_w()
-        c_raw = [load_rows(f"c_raw{a}", tag, c, a) for a, tag in enumerate(("slot2", "slot3"))]
-        gather_words("v_pair", first_picks, (0,))
-        a0 = neighbour_sums(0, "x")
-        gather_words("v_pair_late", late_picks, (1, 2))
-        a1 = neighbour_sums(1, "y")
-
-        round_wc(0, "wc_bf0")
-        first = keep.tile([P, PACK, J], F32, name="first", tag="slot5", align_bytes=64)
-        for t in range(PACK):
-            nc.scalar.copy(out=first[:, t, :], in_=a0[t][:])
-        a2 = neighbour_sums(2, "x")
-        round_wc(1, "slot4")
+        round_scalar(wc_bf[0], wc_raw[0][:])
+        first = relay.tile([P, PARTS, PACK, P], F32, name="first", offset=RAW)
+        for q in range(PARTS):
+            nc.scalar.copy(out=first[:, q, :, :], in_=dealt(a0[q]))
+        a2 = neighbour_sums(2, "x", by_bank)
         quantize_wc(0)
-        second = keep.tile([P, PACK, J], F32, name="second")
-        for t in range(PACK):
-            nc.vector.tensor_tensor(second[:, t, :], a1[t][:], first[:, t, :], ALU.max)
-        c_bf[0] = keep.tile([P, PACK * J], BF16, name="c_bf0", align_bytes=64)
+        second = keep.tile([P, PARTS, PACK, P], F32, name="second")
+        for q in range(PARTS):
+            nc.vector.tensor_tensor(second[:, q, :, :], dealt(a1[q]), first[:, q, :, :], ALU.max)
+        c_bf0 = keep.tile([P, PACK * J], BF16, name="c_bf0", tag="slot2", align_bytes=64)
         for j0 in range(0, J, 256):
-            nc.gpsimd.tensor_scalar(
-                c_bf[0][:, PACK * j0 : PACK * (j0 + 256)].rearrange("p (j i) -> p j i", i=PACK),
-                c_raw[0][:, :, j0 : j0 + 256].rearrange("p i j -> p j i"),
-                1.0,
-                0.0,
-                ALU.mult,
-                ALU.add,
-            )
-        quantize_wc(1)
-        wd_w = keep.tile([P, N], I32, name="wd_w", tag="slot4", align_bytes=64)
+            round_gpsimd(c_bf0[:, PACK * j0 : PACK * (j0 + 256)], c_raw[0][:, :, j0 : j0 + 256])
+        half = R // 2
+        round_scalar(wc_bf[1][:, 0 : PACK * half], wc_raw[1][:, :, 0:half])
+        round_gpsimd(wc_bf[1][:, PACK * half :], wc_raw[1][:, :, half:])
+        quantize_c(c_bf0[:], 0, 0, J)
+        wd_w = keep.tile([P, N], I32, name="wd_w", tag="slot2", align_bytes=64)
         nc.sync.dma_start(out=wd_w[:], in_=wd_words[0].rearrange("p n b -> p (n b)").bitcast(I32))
-        gate = keep.tile([P, N // P, J], F32, name="gate", tag="slot2", align_bytes=64)
+        gate = keep.tile([P, N // P, J], F32, name="gate", tag="slot7", align_bytes=64)
         nc.sync.dma_start(out=gate[:], in_=gm.rearrange("(u p) j -> p u j", p=P))
-        c_w[0] = keep.tile([P, J], U32, name="c_w0", tag="slot5", align_bytes=64)
-        quantize_c(c_bf[0], 0, 0, J)
-        c_w[1] = keep.tile([P, J], U32, name="c_w1", align_bytes=64)
+        quantize_wc(1)
 
+        for q in range(PARTS):
+            (round_gpsimd if q % 2 else round_scalar)(c_parts[q], c_raw[1][:, :, q * P : (q + 1) * P])
         own = []
         for q in range(PARTS):
-            j0, j1 = q * JQ, (q + 1) * JQ
-            c_part = keep.tile([P, PACK * JQ], BF16, name=f"c_part{q}", tag=("slot0", "slot8", "c2", "c3")[q], align_bytes=64)
-            round_c(c_part, 1, j0, j1)
-            quantize_c(c_part, 1, j0, j1)
-            bank = psum.tile([P, PACK, JQ], F32, name=f"own{q}", tag=f"y{q}")
-            for t in range(PACK):
-                for a in range(PASSES):
-                    nc.tensor.matmul_mx(
-                        out=bank[:, t, :],
-                        lhsT=wc_w[a][:, P * t : P * (t + 1)].bitcast(FP8X4),
-                        lhsT_scale=wc_s[a][:, P * t : P * (t + 1)],
-                        rhs=c_w[a][:, j0:j1].bitcast(FP8X4),
-                        rhs_scale=c_s[a][:, j0:j1],
-                        start=(a == 0),
-                        stop=(a == PASSES - 1),
-                    )
+            j0, j1 = q * P, (q + 1) * P
+            quantize_c(c_parts[q], 1, j0, j1)
+            bank = psum.tile([P, R], F32, name=f"own{q}", tag=f"y{q}")
+            for a in range(PASSES):
+                nc.tensor.matmul_mx(
+                    out=bank[:],
+                    lhsT=c_w[a][:, j0:j1].bitcast(FP8X4),
+                    lhsT_scale=c_s[a][:, j0:j1],
+                    rhs=wc_w[a][:].bitcast(FP8X4),
+                    rhs_scale=wc_s[a][:],
+                    start=(a == 0),
+                    stop=(a == PASSES - 1),
+                )
             own.append(bank)
 
-        pooled = keep.tile([P, PACK, J], F32, name="pooled")
-        for t in range(PACK):
-            nc.vector.tensor_tensor(pooled[:, t, :], a2[t][:], second[:, t, :], ALU.max)
         out_rows = out.rearrange("(u p) j -> p u j", p=P)
         for q in range(PARTS):
-            j0, j1 = q * JQ, (q + 1) * JQ
-            pre = keep.tile([P, PACK, JQ], F32, name=f"pre{q}")
-            nc.vector.tensor_tensor(pre[:], own[q][:], pooled[:, :, j0:j1], ALU.add)
-            h_bf = keep.tile([P, PACK * JQ], BF16, name=f"h_bf{q}", align_bytes=64)
+            j0, j1 = q * P, (q + 1) * P
+            tag = (f"best{q}", f"best{q}", "wc_bf1", "c_part0")[q]
+            best = keep.tile([P, PACK, P], F32, name=f"best{q}", tag=tag, align_bytes=64)
+            nc.vector.tensor_tensor(best[:], dealt(a2[q]), second[:, q, :, :], ALU.max)
+            own_sb = keep.tile([P, PACK, P], F32, name=f"own_sb{q}")
+            if q < BY_TENSOR:
+                nc.scalar.copy(out=own_sb[:], in_=dealt(own[q]))
+                terms = (best, own_sb)
+            else:
+                nc.vector.tensor_tensor(own_sb[:], dealt(own[q]), best[:], ALU.add)
+                terms = (own_sb,)
+            pre = psum.tile([P, PACK, P], F32, name=f"pre{q}", tag=f"x{q}")
+            for n, term in enumerate(terms):
+                for t in range(PACK):
+                    nc.tensor.matmul(
+                        pre[:, t, :],
+                        term[:, t, :],
+                        identity[:],
+                        start=(n == 0),
+                        stop=(n == len(terms) - 1),
+                        is_transpose=True,
+                    )
+            h_bf = keep.tile([P, PACK * P], BF16, name=f"h_bf{q}", align_bytes=64)
             nc.scalar.activation(
-                out=h_bf[:].rearrange("p (b e t) -> p b t e", e=4, t=PACK),
-                in_=pre[:].rearrange("p t (b e) -> p b t e", e=4),
-                func=ACT.Relu,
+                out=h_bf[:].rearrange("p (j t) -> p j t", t=PACK), in_=pre[:].rearrange("p t j -> p j t"), func=ACT.Relu
             )
-            h_w = keep.tile([P, JQ], U32, name=f"h_w{q}", align_bytes=64)
-            h_s = keep.tile([P, JQ], U8, name=f"h_s{q}", align_bytes=64)
+            h_w = keep.tile([P, P], U32, name=f"h_w{q}", align_bytes=64)
+            h_s = keep.tile([P, P], U8, name=f"h_s{q}", align_bytes=64)
             nc.vector.quantize_mx(out=h_w[:].bitcast(FP8X4), scales=h_s[:], in_=h_bf[:])
-            bank = psum.tile([P, N // P, JQ], F32, name=f"y{q}", tag=f"x{q}")
+            bank = psum.tile([P, N // P, P], F32, name=f"y{q}", tag=f"y{q}")
             for u in range(N // P):
                 nc.tensor.matmul_mx(
                     out=bank[:, u, :],
                     lhsT=wd_w[:, P * u : P * (u + 1)].bitcast(FP8X4),
-                    lhsT_scale=planes[:, 0, WD_COL + P * u : WD_COL + P * (u + 1)],
+                    lhsT_scale=planes[:, u, WD_COL:PLANE],
                     rhs=h_w[:].bitcast(FP8X4),
                     rhs_scale=h_s[:],
                     start=True,
                     stop=True,
                 )
-            res = keep.tile([P, N // P, JQ], F32, name=f"res{q}")
+            res = keep.tile([P, N // P, P], F32, name=f"res{q}")
             nc.vector.tensor_tensor(res[:], bank[:], gate[:, :, j0:j1], ALU.mult)
             nc.sync.dma_start(out=out_rows[:, :, j0:j1], in_=res[:])

@@ -29,7 +29,6 @@ W_COL = EARLY * J
 WD_COL = W_COL + R
 PLANE = WD_COL + P
 RAW = PACK * J * 4
-BY_TENSOR = 0
 
 
 def tile_list_pnet_gate_kernel(
@@ -130,11 +129,10 @@ def tile_list_pnet_gate_kernel(
             return banks
 
         def dealt(bank):
-            return bank[:].rearrange("p (m t) -> p t m", t=PACK)
+            return bank[:].rearrange("p (m u e) -> p u m e", u=2, e=2)
 
-        by_pass = [(q, a) for a in range(PASSES) for q in range(PARTS)]
         by_bank = [(q, a) for q in range(PARTS) for a in range(PASSES)]
-        a0 = neighbour_sums(0, "x", by_pass)
+        a0 = neighbour_sums(0, "x", by_bank)
         a1 = neighbour_sums(1, "y", by_bank)
 
         wc_w = [
@@ -165,21 +163,24 @@ def tile_list_pnet_gate_kernel(
         def quantize_c(src, a, j0, j1):
             nc.vector.quantize_mx(out=c_w[a][:, j0:j1].bitcast(FP8X4), scales=c_s[a][:, j0:j1], in_=src)
 
-        round_scalar(wc_bf[0], wc_raw[0][:])
-        first = relay.tile([P, PARTS, PACK, P], F32, name="first", offset=RAW)
+        first = keep.tile([P, PARTS, 2, P, 2], F32, name="first")
         for q in range(PARTS):
-            nc.scalar.copy(out=first[:, q, :, :], in_=dealt(a0[q]))
+            nc.scalar.copy(out=first[:, q], in_=dealt(a0[q]))
         a2 = neighbour_sums(2, "x", by_bank)
-        quantize_wc(0)
-        second = keep.tile([P, PARTS, PACK, P], F32, name="second")
-        for q in range(PARTS):
-            nc.vector.tensor_tensor(second[:, q, :, :], dealt(a1[q]), first[:, q, :, :], ALU.max)
-        c_bf0 = keep.tile([P, PACK * J], BF16, name="c_bf0", tag="slot2", align_bytes=64)
-        for j0 in range(0, J, 256):
-            round_gpsimd(c_bf0[:, PACK * j0 : PACK * (j0 + 256)], c_raw[0][:, :, j0 : j0 + 256])
         half = R // 2
-        round_scalar(wc_bf[1][:, 0 : PACK * half], wc_raw[1][:, :, 0:half])
-        round_gpsimd(wc_bf[1][:, PACK * half :], wc_raw[1][:, :, half:])
+        round_scalar(wc_bf[0][:, 0 : PACK * half], wc_raw[0][:, :, 0:half])
+        nc.vector.tensor_copy(
+            wc_bf[0][:, PACK * half :].rearrange("p (b e i) -> p b i e", e=4, i=PACK),
+            wc_raw[0][:, :, half:].rearrange("p i (b e) -> p b i e", e=4),
+        )
+        second = keep.tile([P, PARTS, 2, P, 2], F32, name="second")
+        for q in range(PARTS):
+            nc.vector.tensor_tensor(second[:, q], dealt(a1[q]), first[:, q], ALU.max)
+        quantize_wc(0)
+        c_bf0 = keep.tile([P, PACK * J], BF16, name="c_bf0", tag="slot2", align_bytes=64)
+        for j0 in range(0, J, P):
+            round_gpsimd(c_bf0[:, PACK * j0 : PACK * (j0 + P)], c_raw[0][:, :, j0 : j0 + P])
+        round_scalar(wc_bf[1], wc_raw[1][:])
         quantize_c(c_bf0[:], 0, 0, J)
         wd_w = keep.tile([P, N], I32, name="wd_w", tag="slot2", align_bytes=64)
         nc.sync.dma_start(out=wd_w[:], in_=wd_words[0].rearrange("p n b -> p (n b)").bitcast(I32))
@@ -188,7 +189,7 @@ def tile_list_pnet_gate_kernel(
         quantize_wc(1)
 
         for q in range(PARTS):
-            (round_gpsimd if q % 2 else round_scalar)(c_parts[q], c_raw[1][:, :, q * P : (q + 1) * P])
+            round_scalar(c_parts[q], c_raw[1][:, :, q * P : (q + 1) * P])
         own = []
         for q in range(PARTS):
             j0, j1 = q * P, (q + 1) * P
@@ -207,33 +208,24 @@ def tile_list_pnet_gate_kernel(
             own.append(bank)
 
         out_rows = out.rearrange("(u p) j -> p u j", p=P)
+        h_parts = []
         for q in range(PARTS):
-            j0, j1 = q * P, (q + 1) * P
             tag = (f"best{q}", f"best{q}", "wc_bf1", "c_part0")[q]
-            best = keep.tile([P, PACK, P], F32, name=f"best{q}", tag=tag, align_bytes=64)
-            nc.vector.tensor_tensor(best[:], dealt(a2[q]), second[:, q, :, :], ALU.max)
-            own_sb = keep.tile([P, PACK, P], F32, name=f"own_sb{q}")
-            if q < BY_TENSOR:
-                nc.scalar.copy(out=own_sb[:], in_=dealt(own[q]))
-                terms = (best, own_sb)
-            else:
-                nc.vector.tensor_tensor(own_sb[:], dealt(own[q]), best[:], ALU.add)
-                terms = (own_sb,)
-            pre = psum.tile([P, PACK, P], F32, name=f"pre{q}", tag=f"x{q}")
-            for n, term in enumerate(terms):
-                for t in range(PACK):
-                    nc.tensor.matmul(
-                        pre[:, t, :],
-                        term[:, t, :],
-                        identity[:],
-                        start=(n == 0),
-                        stop=(n == len(terms) - 1),
-                        is_transpose=True,
-                    )
+            best = keep.tile([P, 2, P, 2], F32, name=f"best{q}", tag=tag, align_bytes=64)
+            nc.vector.tensor_tensor(best[:], dealt(a2[q]), second[:, q], ALU.max)
+            own_sb = keep.tile([P, 2, P, 2], BF16, name=f"own_sb{q}")
+            nc.vector.tensor_tensor(own_sb[:], dealt(own[q]), best[:], ALU.add)
+            pre = psum.tile([P, 2, P], F32, name=f"pre{q}", tag=f"x{q}")
+            for u in range(2):
+                nc.tensor.transpose(pre[:, u, :], own_sb[:, u].rearrange("p m e -> p (m e)").bitcast(F32), identity[:])
             h_bf = keep.tile([P, PACK * P], BF16, name=f"h_bf{q}", align_bytes=64)
-            nc.scalar.activation(
-                out=h_bf[:].rearrange("p (j t) -> p j t", t=PACK), in_=pre[:].rearrange("p t j -> p j t"), func=ACT.Relu
-            )
+            h_out = h_bf[:].rearrange("p (j u e) -> p j u e", u=2, e=2)
+            h_in = pre[:].bitcast(BF16).rearrange("p u (j e) -> p j u e", e=2)
+            nc.scalar.activation(out=h_out, in_=h_in, func=ACT.Relu)
+            h_parts.append(h_bf)
+
+        def second_layer(q):
+            h_bf = h_parts[q]
             h_w = keep.tile([P, P], U32, name=f"h_w{q}", align_bytes=64)
             h_s = keep.tile([P, P], U8, name=f"h_s{q}", align_bytes=64)
             nc.vector.quantize_mx(out=h_w[:].bitcast(FP8X4), scales=h_s[:], in_=h_bf[:])
@@ -248,6 +240,16 @@ def tile_list_pnet_gate_kernel(
                     start=True,
                     stop=True,
                 )
+            return bank
+
+        def gate_and_store(q, bank):
+            j0, j1 = q * P, (q + 1) * P
             res = keep.tile([P, N // P, P], F32, name=f"res{q}")
             nc.vector.tensor_tensor(res[:], bank[:], gate[:, :, j0:j1], ALU.mult)
             nc.sync.dma_start(out=out_rows[:, :, j0:j1], in_=res[:])
+
+        y = [second_layer(0)]
+        for q in range(1, PARTS):
+            y.append(second_layer(q))
+            gate_and_store(q - 1, y[q - 1])
+        gate_and_store(PARTS - 1, y[PARTS - 1])

@@ -21,14 +21,16 @@ ACT = mybir.ActivationFunctionType
 P = 128
 PACK = 4
 PASSES = K // (P * PACK)
-QUADS = 4
 PARTS = J // P
-ROWS = slice(96, 128)
+QUADS = 4
+COMPACT = 96
+ROWS = slice(COMPACT, P)
 EARLY = 2
 W_COL = EARLY * J
 WD_COL = W_COL + R
 PLANE = WD_COL + P
 RAW = PACK * J * 4
+RUN = 4
 
 
 def tile_list_pnet_gate_kernel(
@@ -43,59 +45,55 @@ def tile_list_pnet_gate_kernel(
         offsets = keep.tile([P, LISTS * J // 16], U16, name="offsets")
         nc.sync.dma_start(offsets[:], offs)
 
-        tab_s = keep.tile([P, T], U8, name="tab_s", tag="slot0", align_bytes=64)
+        tab_s = keep.tile([P, T], U8, name="tab_s", tag="tab_s", align_bytes=64)
         planes = keep.tile([P, PASSES, PLANE], U8, name="planes", align_bytes=64)
         planes_late = keep.tile([P, PASSES, J], U8, name="planes_late", align_bytes=64)
-        rows_s = keep.tile([P, PLANE], U8, name="rows_s", tag="slot3", align_bytes=64)
+        rows_s = keep.tile([P, PLANE], U8, name="rows_s", tag="rows_s", align_bytes=64)
         identity = keep.tile([P, P], F32, name="identity")
-        nc.vector.memset(tab_s[0:96, :].bitcast(I32), 0)
+        nc.vector.memset(tab_s[0:COMPACT, :].bitcast(I32), 0)
         nc.gpsimd.memset(planes[:].bitcast(I32), 0)
         nc.gpsimd.memset(planes_late[:].bitcast(I32), 0)
         make_identity(nc, identity[:])
 
-        nc.scalar.dma_start(out=tab_s[ROWS, :].bitcast(I32), in_=tab_scales.rearrange("a q t -> q a t").bitcast(I32))
+        nc.scalar.dma_start(out=tab_s[ROWS, :].bitcast(I32), in_=tab_scales.rearrange("a s t -> s a t").bitcast(I32))
         nc.sync.dma_start(
-            out=rows_s[ROWS, W_COL:WD_COL].bitcast(I32), in_=w_scales.rearrange("a q r -> q a r").bitcast(I32)
+            out=rows_s[ROWS, W_COL:WD_COL].bitcast(I32), in_=w_scales.rearrange("a s r -> s a r").bitcast(I32)
         )
         nc.scalar.dma_start(
             out=rows_s[ROWS, WD_COL:PLANE].bitcast(I32),
-            in_=wd_scales[0].rearrange("q (u n) -> (q u) n", n=P).bitcast(I32),
+            in_=wd_scales[0].rearrange("s (b n) -> (s b) n", n=P).bitcast(I32),
         )
-        tab_w = keep.tile([P, T], I32, name="tab_w", tag="slot7", align_bytes=64)
+        tab_w = keep.tile([P, T], I32, name="tab_w", tag="tab_w", align_bytes=64)
         nc.sync.dma_start(out=tab_w[:], in_=tab_words[0].rearrange("p t b -> p (t b)").bitcast(I32))
         w_w = keep.tile([P, PASSES, 2 * R], U8, name="w_w", align_bytes=64)
         nc.sync.dma_start(out=w_w[:].bitcast(I32), in_=w_words.rearrange("a p n -> p a n").bitcast(I32))
 
-        warm = keep.tile([P, 2], F32, name="warm")
-        nc.vector.memset(warm[:, 0:1], 0.0)
-        nc.scalar.activation(out=warm[:, 1:2], in_=warm[:, 0:1], func=ACT.Relu)
-
-        def load_rows(raw, src, a):
+        def load_pass(raw, src, a):
             rows = src[a * P * PACK : (a + 1) * P * PACK, :]
             nc.sync.dma_start(out=raw[:], in_=rows.rearrange("(p i) n -> p i n", i=PACK))
             return raw
 
         def spread_rows(dst, rows):
-            for q in range(QUADS):
+            for quad in range(QUADS):
                 nc.sync.dma_start(
-                    out=dst[32 * q : 32 * q + 4, :, :].bitcast(I32),
-                    in_=rows[96 + 8 * q : 96 + 8 * q + 8, :].bitcast(I32),
+                    out=dst[32 * quad : 32 * quad + 4, :, :].bitcast(I32),
+                    in_=rows[COMPACT + 8 * quad : COMPACT + 8 * quad + 8, :].bitcast(I32),
                 )
 
         v_rows = relay.tile([P, W_COL], U8, name="v_rows", offset=RAW - J)
         nc.vector.tensor_copy(v_rows[:], tab_s[:].indirect(offsets[:, 0 : W_COL // 16]))
         nc.vector.tensor_copy(rows_s[ROWS, 0:W_COL].bitcast(I32), v_rows[ROWS, :].bitcast(I32))
         spread_rows(planes, rows_s)
-        wc_raw = [load_rows(relay.tile([P, PACK, R], F32, name="wc_raw0", offset=RAW), wc, 0)]
+        wc_raw = [load_pass(relay.tile([P, PACK, R], F32, name="wc_raw0", offset=RAW), wc, 0)]
         v_rows_late = relay.tile([P, J], U8, name="v_rows_late", offset=RAW - J)
         nc.vector.tensor_copy(v_rows_late[:], tab_s[:].indirect(offsets[:, W_COL // 16 :]))
         spread_rows(planes_late, v_rows_late)
-        c_raw = [load_rows(keep.tile([P, PACK, J], F32, name="c_raw0", tag="slot0", align_bytes=64), c, 0)]
-        wc_raw.append(load_rows(keep.tile([P, PACK, R], F32, name="wc_raw1", tag="slot3", align_bytes=64), wc, 1))
-        c_raw.append(load_rows(relay.tile([P, PACK, J], F32, name="c_raw1", offset=0), c, 1))
-
+        c_raw = [load_pass(keep.tile([P, PACK, J], F32, name="c_raw0", tag="tab_s", align_bytes=64), c, 0)]
+        wc_raw.append(load_pass(keep.tile([P, PACK, R], F32, name="wc_raw1", tag="rows_s", align_bytes=64), wc, 1))
+        c_raw.append(load_pass(relay.tile([P, PACK, J], F32, name="c_raw1", offset=0), c, 1))
         v_planes = (planes[:, :, 0:J], planes[:, :, J : 2 * J], planes_late[:])
-        first_pair = keep.tile([P, J], U32, name="first_pair", tag="slot2", align_bytes=64)
+
+        first_pair = keep.tile([P, J], U32, name="first_pair", tag="pair", align_bytes=64)
         nc.vector.tensor_copy(first_pair[:], tab_w[:].bitcast(U32).indirect(offsets[:, 0 : J // 16]))
         v_first = []
         for a in range(PASSES):
@@ -103,7 +101,7 @@ def tile_list_pnet_gate_kernel(
             nc.vector.tensor_copy(v_first[a][:].bitcast(U16), first_pair[:].bitcast(U16)[:, a :: PASSES])
         v_w = [[v_first[a][:] for a in range(PASSES)]]
 
-        late_pair = keep.tile([P, LISTS - 1, J], U32, name="late_pair", tag="slot2", align_bytes=64)
+        late_pair = keep.tile([P, LISTS - 1, J], U32, name="late_pair", tag="pair", align_bytes=64)
         nc.vector.tensor_copy(
             late_pair[:].rearrange("p g j -> p (g j)"), tab_w[:].bitcast(U32).indirect(offsets[:, J // 16 :])
         )
@@ -114,92 +112,89 @@ def tile_list_pnet_gate_kernel(
             )
             v_w.append([parted[:, a, :] for a in range(PASSES)])
 
-        def neighbour_sums(g, tag, order):
+        def neighbour_sums(g, tag):
             banks = [psum.tile([P, R], F32, name=f"a{g}_{q}", tag=f"{tag}{q}") for q in range(PARTS)]
-            for q, a in order:
-                nc.tensor.matmul_mx(
-                    out=banks[q][:],
-                    lhsT=v_w[g][a][:, 2 * P * q : 2 * P * (q + 1)].bitcast(FP4X4),
-                    lhsT_scale=v_planes[g][:, a, P * q : P * (q + 1)],
-                    rhs=w_w[:, a, :].bitcast(FP4X4),
-                    rhs_scale=planes[:, a, W_COL:WD_COL],
-                    start=(a == 0),
-                    stop=(a == PASSES - 1),
-                )
+            for q in range(PARTS):
+                for a in range(PASSES):
+                    nc.tensor.matmul_mx(
+                        out=banks[q][:],
+                        lhsT=v_w[g][a][:, 2 * P * q : 2 * P * (q + 1)].bitcast(FP4X4),
+                        lhsT_scale=v_planes[g][:, a, P * q : P * (q + 1)],
+                        rhs=w_w[:, a, :].bitcast(FP4X4),
+                        rhs_scale=planes[:, a, W_COL:WD_COL],
+                        start=(a == 0),
+                        stop=(a == PASSES - 1),
+                    )
             return banks
 
         def dealt(bank):
             return bank[:].rearrange("p (m u e) -> p u m e", u=2, e=2)
 
-        by_bank = [(q, a) for q in range(PARTS) for a in range(PASSES)]
-        a0 = neighbour_sums(0, "x", by_bank)
-        a1 = neighbour_sums(1, "y", by_bank)
+        a0 = neighbour_sums(0, "x")
+        a1 = neighbour_sums(1, "y")
 
-        wc_w = [
-            keep.tile([P, R], U32, name="wc_w0", align_bytes=64),
-            keep.tile([P, R], U32, name="wc_w1", align_bytes=64),
-        ]
+        wc_w = [keep.tile([P, R], U32, name=f"wc_w{a}", align_bytes=64) for a in range(PASSES)]
         wc_s = [keep.tile([P, R], U8, name=f"wc_s{a}", align_bytes=64) for a in range(PASSES)]
         c_w = [keep.tile([P, J], U32, name=f"c_w{a}", align_bytes=64) for a in range(PASSES)]
         c_s = [keep.tile([P, J], U8, name=f"c_s{a}", align_bytes=64) for a in range(PASSES)]
-
         wc_bf = [keep.tile([P, PACK * R], BF16, name=f"wc_bf{a}", align_bytes=64)[:] for a in range(PASSES)]
         c_parts = [keep.tile([P, PACK * P], BF16, name=f"c_part{q}", align_bytes=64)[:] for q in range(PARTS)]
 
-        def round_scalar(dst, raw):
-            nc.scalar.copy(
-                out=dst.rearrange("p (b e i) -> p b i e", e=4, i=PACK),
-                in_=raw.rearrange("p i (b e) -> p b i e", e=4),
+        def in_runs(dst, raw):
+            return (
+                dst.rearrange("p (b n i) -> p b i n", n=RUN, i=PACK),
+                raw.rearrange("p i (b n) -> p b i n", n=RUN),
             )
+
+        def round_scalar(dst, raw):
+            dst_runs, raw_runs = in_runs(dst, raw)
+            nc.scalar.copy(out=dst_runs, in_=raw_runs)
 
         def round_gpsimd(dst, raw):
             nc.gpsimd.tensor_scalar(
-                dst.rearrange("p (j i) -> p j i", i=PACK), raw.rearrange("p i j -> p j i"), 1.0, 0.0, ALU.mult, ALU.add
+                dst.rearrange("p (n i) -> p n i", i=PACK), raw.rearrange("p i n -> p n i"), 1.0, 0.0, ALU.mult, ALU.add
             )
 
-        def quantize_wc(a):
-            nc.vector.quantize_mx(out=wc_w[a][:].bitcast(FP8X4), scales=wc_s[a][:], in_=wc_bf[a])
-
-        def quantize_c(src, a, j0, j1):
-            nc.vector.quantize_mx(out=c_w[a][:, j0:j1].bitcast(FP8X4), scales=c_s[a][:, j0:j1], in_=src)
+        def quantize(words, scales, src):
+            nc.vector.quantize_mx(out=words.bitcast(FP8X4), scales=scales, in_=src)
 
         first = keep.tile([P, PARTS, 2, P, 2], F32, name="first")
         for q in range(PARTS):
             nc.scalar.copy(out=first[:, q], in_=dealt(a0[q]))
-        a2 = neighbour_sums(2, "x", by_bank)
+        a2 = neighbour_sums(2, "x")
+
         half = R // 2
         round_scalar(wc_bf[0][:, 0 : PACK * half], wc_raw[0][:, :, 0:half])
-        nc.vector.tensor_copy(
-            wc_bf[0][:, PACK * half :].rearrange("p (b e i) -> p b i e", e=4, i=PACK),
-            wc_raw[0][:, :, half:].rearrange("p i (b e) -> p b i e", e=4),
-        )
+        nc.vector.tensor_copy(*in_runs(wc_bf[0][:, PACK * half :], wc_raw[0][:, :, half:]))
         second = keep.tile([P, PARTS, 2, P, 2], F32, name="second")
         for q in range(PARTS):
             nc.vector.tensor_tensor(second[:, q], dealt(a1[q]), first[:, q], ALU.max)
-        quantize_wc(0)
-        c_bf0 = keep.tile([P, PACK * J], BF16, name="c_bf0", tag="slot2", align_bytes=64)
-        for j0 in range(0, J, P):
-            round_gpsimd(c_bf0[:, PACK * j0 : PACK * (j0 + P)], c_raw[0][:, :, j0 : j0 + P])
+        quantize(wc_w[0][:], wc_s[0][:], wc_bf[0])
+
+        c_bf0 = keep.tile([P, PACK * J], BF16, name="c_bf0", tag="pair", align_bytes=64)
+        for q in range(PARTS):
+            round_gpsimd(c_bf0[:, PACK * P * q : PACK * P * (q + 1)], c_raw[0][:, :, P * q : P * (q + 1)])
         round_scalar(wc_bf[1], wc_raw[1][:])
-        quantize_c(c_bf0[:], 0, 0, J)
-        wd_w = keep.tile([P, N], I32, name="wd_w", tag="slot2", align_bytes=64)
+        quantize(c_w[0][:], c_s[0][:], c_bf0[:])
+
+        wd_w = keep.tile([P, N], I32, name="wd_w", tag="pair", align_bytes=64)
         nc.sync.dma_start(out=wd_w[:], in_=wd_words[0].rearrange("p n b -> p (n b)").bitcast(I32))
-        gate = keep.tile([P, N // P, J], F32, name="gate", tag="slot7", align_bytes=64)
-        nc.sync.dma_start(out=gate[:], in_=gm.rearrange("(u p) j -> p u j", p=P))
-        quantize_wc(1)
+        gate = keep.tile([P, N // P, J], F32, name="gate", tag="tab_w", align_bytes=64)
+        nc.sync.dma_start(out=gate[:], in_=gm.rearrange("(b p) j -> p b j", p=P))
+        quantize(wc_w[1][:], wc_s[1][:], wc_bf[1])
 
         for q in range(PARTS):
             round_scalar(c_parts[q], c_raw[1][:, :, q * P : (q + 1) * P])
         own = []
         for q in range(PARTS):
-            j0, j1 = q * P, (q + 1) * P
-            quantize_c(c_parts[q], 1, j0, j1)
+            cols = slice(q * P, (q + 1) * P)
+            quantize(c_w[1][:, cols], c_s[1][:, cols], c_parts[q])
             bank = psum.tile([P, R], F32, name=f"own{q}", tag=f"y{q}")
             for a in range(PASSES):
                 nc.tensor.matmul_mx(
                     out=bank[:],
-                    lhsT=c_w[a][:, j0:j1].bitcast(FP8X4),
-                    lhsT_scale=c_s[a][:, j0:j1],
+                    lhsT=c_w[a][:, cols].bitcast(FP8X4),
+                    lhsT_scale=c_s[a][:, cols],
                     rhs=wc_w[a][:].bitcast(FP8X4),
                     rhs_scale=wc_s[a][:],
                     start=(a == 0),
@@ -207,34 +202,36 @@ def tile_list_pnet_gate_kernel(
                 )
             own.append(bank)
 
-        out_rows = out.rearrange("(u p) j -> p u j", p=P)
+        best_tags = ("best0", "best1", "wc_bf1", "c_part0")
+        out_rows = out.rearrange("(b p) j -> p b j", p=P)
         h_parts = []
         for q in range(PARTS):
-            tag = (f"best{q}", f"best{q}", "wc_bf1", "c_part0")[q]
-            best = keep.tile([P, 2, P, 2], F32, name=f"best{q}", tag=tag, align_bytes=64)
+            best = keep.tile([P, 2, P, 2], F32, name=f"best{q}", tag=best_tags[q], align_bytes=64)
             nc.vector.tensor_tensor(best[:], dealt(a2[q]), second[:, q], ALU.max)
-            own_sb = keep.tile([P, 2, P, 2], BF16, name=f"own_sb{q}")
-            nc.vector.tensor_tensor(own_sb[:], dealt(own[q]), best[:], ALU.add)
-            pre = psum.tile([P, 2, P], F32, name=f"pre{q}", tag=f"x{q}")
+            summed = keep.tile([P, 2, P, 2], BF16, name=f"summed{q}")
+            nc.vector.tensor_tensor(summed[:], dealt(own[q]), best[:], ALU.add)
+            turned = psum.tile([P, 2, P], F32, name=f"turned{q}", tag=f"x{q}")
             for u in range(2):
-                nc.tensor.transpose(pre[:, u, :], own_sb[:, u].rearrange("p m e -> p (m e)").bitcast(F32), identity[:])
+                pair_words = summed[:, u].rearrange("p m e -> p (m e)").bitcast(F32)
+                nc.tensor.transpose(turned[:, u, :], pair_words, identity[:])
             h_bf = keep.tile([P, PACK * P], BF16, name=f"h_bf{q}", align_bytes=64)
-            h_out = h_bf[:].rearrange("p (j u e) -> p j u e", u=2, e=2)
-            h_in = pre[:].bitcast(BF16).rearrange("p u (j e) -> p j u e", e=2)
-            nc.scalar.activation(out=h_out, in_=h_in, func=ACT.Relu)
+            nc.scalar.activation(
+                out=h_bf[:].rearrange("p (j u e) -> p j u e", u=2, e=2),
+                in_=turned[:].bitcast(BF16).rearrange("p u (j e) -> p j u e", e=2),
+                func=ACT.Relu,
+            )
             h_parts.append(h_bf)
 
         def second_layer(q):
-            h_bf = h_parts[q]
             h_w = keep.tile([P, P], U32, name=f"h_w{q}", align_bytes=64)
             h_s = keep.tile([P, P], U8, name=f"h_s{q}", align_bytes=64)
-            nc.vector.quantize_mx(out=h_w[:].bitcast(FP8X4), scales=h_s[:], in_=h_bf[:])
+            quantize(h_w[:], h_s[:], h_parts[q][:])
             bank = psum.tile([P, N // P, P], F32, name=f"y{q}", tag=f"y{q}")
-            for u in range(N // P):
+            for b in range(N // P):
                 nc.tensor.matmul_mx(
-                    out=bank[:, u, :],
-                    lhsT=wd_w[:, P * u : P * (u + 1)].bitcast(FP8X4),
-                    lhsT_scale=planes[:, u, WD_COL:PLANE],
+                    out=bank[:, b, :],
+                    lhsT=wd_w[:, P * b : P * (b + 1)].bitcast(FP8X4),
+                    lhsT_scale=planes[:, b, WD_COL:PLANE],
                     rhs=h_w[:].bitcast(FP8X4),
                     rhs_scale=h_s[:],
                     start=True,
@@ -243,10 +240,10 @@ def tile_list_pnet_gate_kernel(
             return bank
 
         def gate_and_store(q, bank):
-            j0, j1 = q * P, (q + 1) * P
+            cols = slice(q * P, (q + 1) * P)
             res = keep.tile([P, N // P, P], F32, name=f"res{q}")
-            nc.vector.tensor_tensor(res[:], bank[:], gate[:, :, j0:j1], ALU.mult)
-            nc.sync.dma_start(out=out_rows[:, :, j0:j1], in_=res[:])
+            nc.vector.tensor_tensor(res[:], bank[:], gate[:, :, cols], ALU.mult)
+            nc.sync.dma_start(out=out_rows[:, :, cols], in_=res[:])
 
         y = [second_layer(0)]
         for q in range(1, PARTS):

@@ -95,43 +95,45 @@ def tile_list_pnet_gate_kernel(
 
         first_pair = keep.tile([P, J], U32, name="first_pair", tag="pair", align_bytes=64)
         nc.vector.tensor_copy(first_pair[:], tab_w[:].bitcast(U32).indirect(offsets[:, 0 : J // 16]))
-        v_first = []
-        for a in range(PASSES):
-            v_first.append(keep.tile([P, 2 * J], U8, name=f"v_first{a}", align_bytes=64))
-            nc.vector.tensor_copy(v_first[a][:].bitcast(U16), first_pair[:].bitcast(U16)[:, a :: PASSES])
-        v_w = [[v_first[a][:] for a in range(PASSES)]]
+        halves = first_pair[:].bitcast(U16).rearrange("p (j a) -> p a j", a=PASSES)
+        v_head = keep.tile([P, PASSES, 2 * P], U8, name="v_head", align_bytes=64)
+        v_rest = keep.tile([P, PASSES, 2 * (J - P)], U8, name="v_rest", align_bytes=64)
+        nc.vector.tensor_copy(v_head[:].bitcast(U16), halves[:, :, 0:P])
+        nc.vector.tensor_copy(v_rest[:].bitcast(U16), halves[:, :, P:])
+        v_w = [[v_head[:]] + [v_rest[:, :, 2 * P * q : 2 * P * (q + 1)] for q in range(PARTS - 1)]]
 
         late_pair = keep.tile([P, LISTS - 1, J], U32, name="late_pair", tag="pair", align_bytes=64)
-        nc.vector.tensor_copy(
-            late_pair[:].rearrange("p g j -> p (g j)"), tab_w[:].bitcast(U32).indirect(offsets[:, J // 16 :])
-        )
+        for g in range(1, LISTS):
+            listed = offsets[:, g * J // 16 : (g + 1) * J // 16]
+            nc.vector.tensor_copy(late_pair[:, g - 1, :], tab_w[:].bitcast(U32).indirect(listed))
         for g in range(1, LISTS):
             parted = keep.tile([P, PASSES, 2 * J], U8, name=f"v_late{g}", align_bytes=64)
             nc.vector.tensor_copy(
                 parted[:].bitcast(U16), late_pair[:, g - 1, :].bitcast(U16).rearrange("p (j a) -> p a j", a=PASSES)
             )
-            v_w.append([parted[:, a, :] for a in range(PASSES)])
+            v_w.append([parted[:, :, 2 * P * q : 2 * P * (q + 1)] for q in range(PARTS)])
 
-        def neighbour_sums(g, tag):
-            banks = [psum.tile([P, R], F32, name=f"a{g}_{q}", tag=f"{tag}{q}") for q in range(PARTS)]
-            for q in range(PARTS):
-                for a in range(PASSES):
-                    nc.tensor.matmul_mx(
-                        out=banks[q][:],
-                        lhsT=v_w[g][a][:, 2 * P * q : 2 * P * (q + 1)].bitcast(FP4X4),
-                        lhsT_scale=v_planes[g][:, a, P * q : P * (q + 1)],
-                        rhs=w_w[:, a, :].bitcast(FP4X4),
-                        rhs_scale=planes[:, a, W_COL:WD_COL],
-                        start=(a == 0),
-                        stop=(a == PASSES - 1),
-                    )
-            return banks
+        def neighbour_sum(g, q, tag):
+            bank = psum.tile([P, R], F32, name=f"a{g}_{q}", tag=f"{tag}{q}")
+            for a in range(PASSES):
+                nc.tensor.matmul_mx(
+                    out=bank[:],
+                    lhsT=v_w[g][q][:, a, :].bitcast(FP4X4),
+                    lhsT_scale=v_planes[g][:, a, P * q : P * (q + 1)],
+                    rhs=w_w[:, a, :].bitcast(FP4X4),
+                    rhs_scale=planes[:, a, W_COL:WD_COL],
+                    start=(a == 0),
+                    stop=(a == PASSES - 1),
+                )
+            return bank
 
         def dealt(bank):
             return bank[:].rearrange("p (m u e) -> p u m e", u=2, e=2)
 
-        a0 = neighbour_sums(0, "x")
-        a1 = neighbour_sums(1, "y")
+        a0 = [neighbour_sum(0, q, "x") for q in range(PARTS - 1)]
+        a1 = [neighbour_sum(1, q, "y") for q in range(PARTS - 1)]
+        a0.append(neighbour_sum(0, PARTS - 1, "x"))
+        a1.append(neighbour_sum(1, PARTS - 1, "y"))
 
         wc_w = [keep.tile([P, R], U32, name=f"wc_w{a}", align_bytes=64) for a in range(PASSES)]
         wc_s = [keep.tile([P, R], U8, name=f"wc_s{a}", align_bytes=64) for a in range(PASSES)]
@@ -158,23 +160,32 @@ def tile_list_pnet_gate_kernel(
         def quantize(words, scales, src):
             nc.vector.quantize_mx(out=words.bitcast(FP8X4), scales=scales, in_=src)
 
-        first = keep.tile([P, PARTS, 2, P, 2], F32, name="first")
+        first = [keep.tile([P, 2, P, 2], F32, name=f"first{q}", align_bytes=64) for q in range(PARTS)]
         for q in range(PARTS):
-            nc.scalar.copy(out=first[:, q], in_=dealt(a0[q]))
-        a2 = neighbour_sums(2, "x")
+            nc.scalar.copy(out=first[q][:], in_=dealt(a0[q]))
+        a2 = [neighbour_sum(2, q, "x") for q in range(PARTS)]
 
         half = R // 2
         round_scalar(wc_bf[0][:, 0 : PACK * half], wc_raw[0][:, :, 0:half])
         nc.vector.tensor_copy(*in_runs(wc_bf[0][:, PACK * half :], wc_raw[0][:, :, half:]))
         second = keep.tile([P, PARTS, 2, P, 2], F32, name="second")
         for q in range(PARTS):
-            nc.vector.tensor_tensor(second[:, q], dealt(a1[q]), first[:, q], ALU.max)
-        quantize(wc_w[0][:], wc_s[0][:], wc_bf[0])
+            if q == PARTS - 1:
+                quantize(wc_w[0][:], wc_s[0][:], wc_bf[0])
+            nc.vector.tensor_tensor(second[:, q], dealt(a1[q]), first[q][:], ALU.max)
 
         c_bf0 = keep.tile([P, PACK * J], BF16, name="c_bf0", tag="pair", align_bytes=64)
         for q in range(PARTS):
             round_gpsimd(c_bf0[:, PACK * P * q : PACK * P * (q + 1)], c_raw[0][:, :, P * q : P * (q + 1)])
         round_scalar(wc_bf[1], wc_raw[1][:])
+        best = []
+
+        def second_max(q, tag):
+            best.append(keep.tile([P, 2, P, 2], F32, name=f"best{q}", tag=tag, align_bytes=64))
+            nc.vector.tensor_tensor(best[q][:], dealt(a2[q]), second[:, q], ALU.max)
+
+        second_max(0, "best0")
+        second_max(1, "best1")
         quantize(c_w[0][:], c_s[0][:], c_bf0[:])
 
         wd_w = keep.tile([P, N], I32, name="wd_w", tag="pair", align_bytes=64)
@@ -202,14 +213,13 @@ def tile_list_pnet_gate_kernel(
                 )
             own.append(bank)
 
-        best_tags = ("best0", "best1", "wc_bf1", "c_part0")
+        second_max(2, "wc_bf1")
+        second_max(3, "c_part0")
         out_rows = out.rearrange("(b p) j -> p b j", p=P)
         h_parts = []
         for q in range(PARTS):
-            best = keep.tile([P, 2, P, 2], F32, name=f"best{q}", tag=best_tags[q], align_bytes=64)
-            nc.vector.tensor_tensor(best[:], dealt(a2[q]), second[:, q], ALU.max)
             summed = keep.tile([P, 2, P, 2], BF16, name=f"summed{q}")
-            nc.vector.tensor_tensor(summed[:], dealt(own[q]), best[:], ALU.add)
+            nc.vector.tensor_tensor(summed[:], dealt(own[q]), best[q][:], ALU.add)
             turned = psum.tile([P, 2, P], F32, name=f"turned{q}", tag=f"x{q}")
             for u in range(2):
                 pair_words = summed[:, u].rearrange("p m e -> p (m e)").bitcast(F32)

@@ -1,7 +1,6 @@
 from contextlib import ExitStack
 
 import concourse.mybir as mybir
-from concourse.masks import make_identity
 
 K, R, N, T, J = 1024, 512, 256, 4096, 512
 LISTS = 3
@@ -22,6 +21,7 @@ P = 128
 PACK = 4
 PASSES = K // (P * PACK)
 PARTS = J // P
+HALF = J // 2
 QUADS = 4
 COMPACT = 96
 ROWS = slice(COMPACT, P)
@@ -43,30 +43,32 @@ def tile_list_pnet_gate_kernel(
         psum = ctx.enter_context(tc.psum_pool(name="psum", bufs=1))
 
         offsets = keep.tile([P, LISTS * J // 16], U16, name="offsets")
-        nc.sync.dma_start(offsets[:], offs)
 
         tab_s = keep.tile([P, T], U8, name="tab_s", tag="tab_s", align_bytes=64)
         planes = keep.tile([P, PASSES, PLANE], U8, name="planes", align_bytes=64)
         planes_late = keep.tile([P, PASSES, J], U8, name="planes_late", align_bytes=64)
         rows_s = keep.tile([P, PLANE], U8, name="rows_s", tag="rows_s", align_bytes=64)
-        identity = keep.tile([P, P], F32, name="identity")
+        w_rows = keep.tile([P, R], U8, name="w_rows", align_bytes=64)
         nc.vector.memset(tab_s[0:COMPACT, :].bitcast(I32), 0)
+        nc.gpsimd.memset(w_rows[0:COMPACT, :].bitcast(I32), 0)
         nc.gpsimd.memset(planes[:].bitcast(I32), 0)
         nc.gpsimd.memset(planes_late[:].bitcast(I32), 0)
-        make_identity(nc, identity[:])
 
+        nc.sync.dma_start(out=w_rows[ROWS, :].bitcast(I32), in_=w_scales.rearrange("a s r -> s a r").bitcast(I32))
+        nc.sync.dma_start(offsets[:], offs)
         nc.scalar.dma_start(out=tab_s[ROWS, :].bitcast(I32), in_=tab_scales.rearrange("a s t -> s a t").bitcast(I32))
-        nc.sync.dma_start(
-            out=rows_s[ROWS, W_COL:WD_COL].bitcast(I32), in_=w_scales.rearrange("a s r -> s a r").bitcast(I32)
-        )
         nc.scalar.dma_start(
             out=rows_s[ROWS, WD_COL:PLANE].bitcast(I32),
             in_=wd_scales[0].rearrange("s (b n) -> (s b) n", n=P).bitcast(I32),
         )
         tab_w = keep.tile([P, T], I32, name="tab_w", tag="tab_w", align_bytes=64)
         nc.sync.dma_start(out=tab_w[:], in_=tab_words[0].rearrange("p t b -> p (t b)").bitcast(I32))
-        w_w = keep.tile([P, PASSES, 2 * R], U8, name="w_w", align_bytes=64)
+        w_w = keep.tile([P, PASSES, 2 * R], U8, name="w_w", tag="pair", align_bytes=64)
         nc.sync.dma_start(out=w_w[:].bitcast(I32), in_=w_words.rearrange("a p n -> p a n").bitcast(I32))
+
+        nc.vector.tensor_copy(
+            rows_s[:, W_COL:WD_COL].rearrange("p (t m) -> p t m", t=PACK), w_rows[:].rearrange("p (m t) -> p t m", t=PACK)
+        )
 
         def load_pass(raw, src, a):
             rows = src[a * P * PACK : (a + 1) * P * PACK, :]
@@ -93,14 +95,19 @@ def tile_list_pnet_gate_kernel(
         c_raw.append(load_pass(relay.tile([P, PACK, J], F32, name="c_raw1", offset=0), c, 1))
         v_planes = (planes[:, :, 0:J], planes[:, :, J : 2 * J], planes_late[:])
 
-        first_pair = keep.tile([P, J], U32, name="first_pair", tag="pair", align_bytes=64)
+        first_pair = keep.tile([P, J], U32, name="first_pair", align_bytes=64)
         nc.vector.tensor_copy(first_pair[:], tab_w[:].bitcast(U32).indirect(offsets[:, 0 : J // 16]))
+        w_dealt = keep.tile([P, PASSES, 2 * R], U8, name="w_dealt", align_bytes=64)
+        nc.vector.tensor_copy(
+            w_dealt[:].bitcast(U16).rearrange("p a (t m) -> p a t m", t=PACK),
+            w_w[:].bitcast(U16).rearrange("p a (m t) -> p a t m", t=PACK),
+        )
         halves = first_pair[:].bitcast(U16).rearrange("p (j a) -> p a j", a=PASSES)
-        v_head = keep.tile([P, PASSES, 2 * P], U8, name="v_head", align_bytes=64)
-        v_rest = keep.tile([P, PASSES, 2 * (J - P)], U8, name="v_rest", align_bytes=64)
-        nc.vector.tensor_copy(v_head[:].bitcast(U16), halves[:, :, 0:P])
-        nc.vector.tensor_copy(v_rest[:].bitcast(U16), halves[:, :, P:])
-        v_w = [[v_head[:]] + [v_rest[:, :, 2 * P * q : 2 * P * (q + 1)] for q in range(PARTS - 1)]]
+        v_w = [[]]
+        for h in range(2):
+            v_half = keep.tile([P, PASSES, 2 * HALF], U8, name=f"v_half{h}", align_bytes=64)
+            nc.vector.tensor_copy(v_half[:].bitcast(U16), halves[:, :, HALF * h : HALF * (h + 1)])
+            v_w[0].append(v_half[:])
 
         late_pair = keep.tile([P, LISTS - 1, J], U32, name="late_pair", tag="pair", align_bytes=64)
         for g in range(1, LISTS):
@@ -111,24 +118,27 @@ def tile_list_pnet_gate_kernel(
             nc.vector.tensor_copy(
                 parted[:].bitcast(U16), late_pair[:, g - 1, :].bitcast(U16).rearrange("p (j a) -> p a j", a=PASSES)
             )
-            v_w.append([parted[:, :, 2 * P * q : 2 * P * (q + 1)] for q in range(PARTS)])
+            v_w.append([parted[:, :, 2 * HALF * h : 2 * HALF * (h + 1)] for h in range(2)])
 
-        def neighbour_sum(g, q, tag):
-            bank = psum.tile([P, R], F32, name=f"a{g}_{q}", tag=f"{tag}{q}")
-            for a in range(PASSES):
-                nc.tensor.matmul_mx(
-                    out=bank[:],
-                    lhsT=v_w[g][q][:, a, :].bitcast(FP4X4),
-                    lhsT_scale=v_planes[g][:, a, P * q : P * (q + 1)],
-                    rhs=w_w[:, a, :].bitcast(FP4X4),
-                    rhs_scale=planes[:, a, W_COL:WD_COL],
-                    start=(a == 0),
-                    stop=(a == PASSES - 1),
-                )
+        def neighbour_sum(g, b, tag):
+            h, u = divmod(b, 2)
+            bank = psum.tile([P, 2, HALF], F32, name=f"a{g}_{b}", tag=f"{tag}{b}")
+            for e in range(2):
+                t = 2 * u + e
+                for a in range(PASSES):
+                    nc.tensor.matmul_mx(
+                        out=bank[:, e, :],
+                        lhsT=w_dealt[:, a, 2 * P * t : 2 * P * (t + 1)].bitcast(FP4X4),
+                        lhsT_scale=planes[:, a, W_COL + P * t : W_COL + P * (t + 1)],
+                        rhs=v_w[g][h][:, a, :].bitcast(FP4X4),
+                        rhs_scale=v_planes[g][:, a, HALF * h : HALF * (h + 1)],
+                        start=(a == 0),
+                        stop=(a == PASSES - 1),
+                    )
             return bank
 
-        def dealt(bank):
-            return bank[:].rearrange("p (m u e) -> p u m e", u=2, e=2)
+        def woven(bank):
+            return bank[:].rearrange("p e j -> p j e")
 
         a0 = [neighbour_sum(0, q, "x") for q in range(PARTS - 1)]
         a1 = [neighbour_sum(1, q, "y") for q in range(PARTS - 1)]
@@ -152,6 +162,12 @@ def tile_list_pnet_gate_kernel(
             dst_runs, raw_runs = in_runs(dst, raw)
             nc.scalar.copy(out=dst_runs, in_=raw_runs)
 
+        def dealt_runs(dst, raw, lo, hi):
+            return (
+                dst[:, PACK * P * lo : PACK * P * hi].rearrange("p (t m i) -> p m i t", m=P, i=PACK),
+                raw.rearrange("p i (m t) -> p m i t", t=PACK)[:, :, :, lo:hi],
+            )
+
         def round_gpsimd(dst, raw):
             nc.gpsimd.tensor_scalar(
                 dst.rearrange("p (n i) -> p n i", i=PACK), raw.rearrange("p i n -> p n i"), 1.0, 0.0, ALU.mult, ALU.add
@@ -160,32 +176,33 @@ def tile_list_pnet_gate_kernel(
         def quantize(words, scales, src):
             nc.vector.quantize_mx(out=words.bitcast(FP8X4), scales=scales, in_=src)
 
-        first = [keep.tile([P, 2, P, 2], F32, name=f"first{q}", align_bytes=64) for q in range(PARTS)]
+        first = [keep.tile([P, HALF, 2], F32, name=f"first{q}", align_bytes=64) for q in range(PARTS)]
         for q in range(PARTS):
-            nc.scalar.copy(out=first[q][:], in_=dealt(a0[q]))
+            nc.scalar.copy(out=first[q][:], in_=woven(a0[q]))
         a2 = [neighbour_sum(2, q, "x") for q in range(PARTS)]
 
-        half = R // 2
-        round_scalar(wc_bf[0][:, 0 : PACK * half], wc_raw[0][:, :, 0:half])
-        nc.vector.tensor_copy(*in_runs(wc_bf[0][:, PACK * half :], wc_raw[0][:, :, half:]))
-        second = keep.tile([P, PARTS, 2, P, 2], F32, name="second")
+        nc.scalar.copy(*dealt_runs(wc_bf[0], wc_raw[0][:], 0, 2))
+        nc.vector.tensor_copy(*dealt_runs(wc_bf[0], wc_raw[0][:], 2, 4))
+        second = keep.tile([P, PARTS, HALF, 2], F32, name="second")
         for q in range(PARTS):
             if q == PARTS - 1:
                 quantize(wc_w[0][:], wc_s[0][:], wc_bf[0])
-            nc.vector.tensor_tensor(second[:, q], dealt(a1[q]), first[q][:], ALU.max)
+            nc.vector.tensor_tensor(second[:, q], woven(a1[q]), first[q][:], ALU.max)
 
         c_bf0 = keep.tile([P, PACK * J], BF16, name="c_bf0", tag="pair", align_bytes=64)
         for q in range(PARTS):
             round_gpsimd(c_bf0[:, PACK * P * q : PACK * P * (q + 1)], c_raw[0][:, :, P * q : P * (q + 1)])
-        round_scalar(wc_bf[1], wc_raw[1][:])
-        best = []
+        nc.scalar.copy(*dealt_runs(wc_bf[1], wc_raw[1][:], 0, 4))
+        best = [
+            keep.tile([P, 2, HALF, 2], F32, name="best0", align_bytes=64),
+            keep.tile([P, 2, HALF, 2], F32, name="best1", tag="wc_bf1", align_bytes=64),
+        ]
 
-        def second_max(q, tag):
-            best.append(keep.tile([P, 2, P, 2], F32, name=f"best{q}", tag=tag, align_bytes=64))
-            nc.vector.tensor_tensor(best[q][:], dealt(a2[q]), second[:, q], ALU.max)
+        def second_max(b):
+            nc.vector.tensor_tensor(best[b // 2][:, b % 2], woven(a2[b]), second[:, b], ALU.max)
 
-        second_max(0, "best0")
-        second_max(1, "best1")
+        second_max(0)
+        second_max(1)
         quantize(c_w[0][:], c_s[0][:], c_bf0[:])
 
         wd_w = keep.tile([P, N], I32, name="wd_w", tag="pair", align_bytes=64)
@@ -200,43 +217,45 @@ def tile_list_pnet_gate_kernel(
         for q in range(PARTS):
             cols = slice(q * P, (q + 1) * P)
             quantize(c_w[1][:, cols], c_s[1][:, cols], c_parts[q])
-            bank = psum.tile([P, R], F32, name=f"own{q}", tag=f"y{q}")
+            bank = psum.tile([P, PACK, P], F32, name=f"own{q}", tag=f"y{q}")
             for a in range(PASSES):
-                nc.tensor.matmul_mx(
-                    out=bank[:],
-                    lhsT=c_w[a][:, cols].bitcast(FP8X4),
-                    lhsT_scale=c_s[a][:, cols],
-                    rhs=wc_w[a][:].bitcast(FP8X4),
-                    rhs_scale=wc_s[a][:],
-                    start=(a == 0),
-                    stop=(a == PASSES - 1),
-                )
+                for t in range(PACK):
+                    nc.tensor.matmul_mx(
+                        out=bank[:, t, :],
+                        lhsT=wc_w[a][:, P * t : P * (t + 1)].bitcast(FP8X4),
+                        lhsT_scale=wc_s[a][:, P * t : P * (t + 1)],
+                        rhs=c_w[a][:, cols].bitcast(FP8X4),
+                        rhs_scale=c_s[a][:, cols],
+                        start=(a == 0 and t == 0),
+                        stop=(a == PASSES - 1 and t == PACK - 1),
+                    )
             own.append(bank)
 
-        second_max(2, "wc_bf1")
-        second_max(3, "c_part0")
+        second_max(2)
+        second_max(3)
         out_rows = out.rearrange("(b p) j -> p b j", p=P)
         h_parts = []
         for q in range(PARTS):
-            summed = keep.tile([P, 2, P, 2], BF16, name=f"summed{q}")
-            nc.vector.tensor_tensor(summed[:], dealt(own[q]), best[q][:], ALU.add)
-            turned = psum.tile([P, 2, P], F32, name=f"turned{q}", tag=f"x{q}")
-            for u in range(2):
-                pair_words = summed[:, u].rearrange("p m e -> p (m e)").bitcast(F32)
-                nc.tensor.transpose(turned[:, u, :], pair_words, identity[:])
-            h_bf = keep.tile([P, PACK * P], BF16, name=f"h_bf{q}", align_bytes=64)
-            nc.scalar.activation(
-                out=h_bf[:].rearrange("p (j u e) -> p j u e", u=2, e=2),
-                in_=turned[:].bitcast(BF16).rearrange("p u (j e) -> p j u e", e=2),
-                func=ACT.Relu,
+            summed = keep.tile([P, PACK * P], BF16, name=f"summed{q}")
+            pooled = best[q // 2][:, :, P * (q % 2) : P * (q % 2 + 1), :]
+            nc.vector.tensor_tensor(
+                summed[:].rearrange("p (j u e) -> p j u e", u=2, e=2),
+                own[q][:].rearrange("p (u e) j -> p j u e", e=2),
+                pooled.rearrange("p u j e -> p j u e"),
+                ALU.add,
             )
+            h_bf = keep.tile([P, PACK * P], BF16, name=f"h_bf{q}", align_bytes=64)
+            if q < PARTS - 1:
+                nc.scalar.activation(out=h_bf[:], in_=summed[:], func=ACT.Relu)
+            else:
+                nc.vector.tensor_scalar_max(h_bf[:], summed[:], 0.0)
             h_parts.append(h_bf)
 
         def second_layer(q):
             h_w = keep.tile([P, P], U32, name=f"h_w{q}", align_bytes=64)
             h_s = keep.tile([P, P], U8, name=f"h_s{q}", align_bytes=64)
             quantize(h_w[:], h_s[:], h_parts[q][:])
-            bank = psum.tile([P, N // P, P], F32, name=f"y{q}", tag=f"y{q}")
+            bank = psum.tile([P, N // P, P], F32, name=f"y{q}", tag=f"x{q}")
             for b in range(N // P):
                 nc.tensor.matmul_mx(
                     out=bank[:, b, :],

@@ -22,6 +22,7 @@ PACK = 4
 PASSES = K // (P * PACK)
 PARTS = J // P
 HALF = J // 2
+BANKS = 4
 QUADS = 4
 COMPACT = 96
 ROWS = slice(COMPACT, P)
@@ -61,13 +62,14 @@ def tile_list_pnet_gate_kernel(
             out=rows_s[ROWS, WD_COL:PLANE].bitcast(I32),
             in_=wd_scales[0].rearrange("s (b n) -> (s b) n", n=P).bitcast(I32),
         )
-        tab_w = keep.tile([P, T], I32, name="tab_w", tag="tab_w", align_bytes=64)
+        tab_w = keep.tile([P, T], I32, name="tab_w", align_bytes=64)
         nc.sync.dma_start(out=tab_w[:], in_=tab_words[0].rearrange("p t b -> p (t b)").bitcast(I32))
         w_w = keep.tile([P, PASSES, 2 * R], U8, name="w_w", tag="pair", align_bytes=64)
         nc.sync.dma_start(out=w_w[:].bitcast(I32), in_=w_words.rearrange("a p n -> p a n").bitcast(I32))
 
         nc.vector.tensor_copy(
-            rows_s[:, W_COL:WD_COL].rearrange("p (t m) -> p t m", t=PACK), w_rows[:].rearrange("p (m t) -> p t m", t=PACK)
+            rows_s[:, W_COL:WD_COL].rearrange("p (t m) -> p t m", t=PACK),
+            w_rows[:].rearrange("p (m t) -> p t m", t=PACK),
         )
 
         def load_pass(raw, src, a):
@@ -82,9 +84,11 @@ def tile_list_pnet_gate_kernel(
                     in_=rows[COMPACT + 8 * quad : COMPACT + 8 * quad + 8, :].bitcast(I32),
                 )
 
-        v_rows = relay.tile([P, W_COL], U8, name="v_rows", offset=RAW - J)
-        nc.vector.tensor_copy(v_rows[:], tab_s[:].indirect(offsets[:, 0 : W_COL // 16]))
-        nc.vector.tensor_copy(rows_s[ROWS, 0:W_COL].bitcast(I32), v_rows[ROWS, :].bitcast(I32))
+        v_rows = [relay.tile([P, J], U8, name=f"v_rows{g}", offset=RAW - J + J * g) for g in range(EARLY)]
+        for g in range(EARLY):
+            nc.vector.tensor_copy(v_rows[g][:], tab_s[:].indirect(offsets[:, g * J // 16 : (g + 1) * J // 16]))
+        for g in range(EARLY):
+            nc.vector.tensor_copy(rows_s[ROWS, g * J : (g + 1) * J].bitcast(I32), v_rows[g][ROWS, :].bitcast(I32))
         spread_rows(planes, rows_s)
         wc_raw = [load_pass(relay.tile([P, PACK, R], F32, name="wc_raw0", offset=RAW), wc, 0)]
         v_rows_late = relay.tile([P, J], U8, name="v_rows_late", offset=RAW - J)
@@ -97,16 +101,17 @@ def tile_list_pnet_gate_kernel(
 
         first_pair = keep.tile([P, J], U32, name="first_pair", align_bytes=64)
         nc.vector.tensor_copy(first_pair[:], tab_w[:].bitcast(U32).indirect(offsets[:, 0 : J // 16]))
-        w_dealt = keep.tile([P, PASSES, 2 * R], U8, name="w_dealt", align_bytes=64)
-        nc.vector.tensor_copy(
-            w_dealt[:].bitcast(U16).rearrange("p a (t m) -> p a t m", t=PACK),
-            w_w[:].bitcast(U16).rearrange("p a (m t) -> p a t m", t=PACK),
-        )
         halves = first_pair[:].bitcast(U16).rearrange("p (j a) -> p a j", a=PASSES)
+        w_cols = w_w[:].bitcast(U16).rearrange("p a (m t) -> p a t m", t=PACK)
+        w_dealt = []
         v_w = [[]]
-        for h in range(2):
-            v_half = keep.tile([P, PASSES, 2 * HALF], U8, name=f"v_half{h}", align_bytes=64)
-            nc.vector.tensor_copy(v_half[:].bitcast(U16), halves[:, :, HALF * h : HALF * (h + 1)])
+        for n in range(2):
+            w_dealt.append(keep.tile([P, PASSES, R], U8, name=f"w_dealt{n}", align_bytes=64))
+            nc.vector.tensor_copy(
+                w_dealt[n][:].bitcast(U16).rearrange("p a (e m) -> p a e m", e=2), w_cols[:, :, 2 * n : 2 * n + 2, :]
+            )
+            v_half = keep.tile([P, PASSES, 2 * HALF], U8, name=f"v_half{n}", align_bytes=64)
+            nc.vector.tensor_copy(v_half[:].bitcast(U16), halves[:, :, HALF * n : HALF * (n + 1)])
             v_w[0].append(v_half[:])
 
         late_pair = keep.tile([P, LISTS - 1, J], U32, name="late_pair", tag="pair", align_bytes=64)
@@ -128,7 +133,7 @@ def tile_list_pnet_gate_kernel(
                 for a in range(PASSES):
                     nc.tensor.matmul_mx(
                         out=bank[:, e, :],
-                        lhsT=w_dealt[:, a, 2 * P * t : 2 * P * (t + 1)].bitcast(FP4X4),
+                        lhsT=w_dealt[u][:, a, 2 * P * e : 2 * P * (e + 1)].bitcast(FP4X4),
                         lhsT_scale=planes[:, a, W_COL + P * t : W_COL + P * (t + 1)],
                         rhs=v_w[g][h][:, a, :].bitcast(FP4X4),
                         rhs_scale=v_planes[g][:, a, HALF * h : HALF * (h + 1)],
@@ -140,10 +145,10 @@ def tile_list_pnet_gate_kernel(
         def woven(bank):
             return bank[:].rearrange("p e j -> p j e")
 
-        a0 = [neighbour_sum(0, q, "x") for q in range(PARTS - 1)]
-        a1 = [neighbour_sum(1, q, "y") for q in range(PARTS - 1)]
-        a0.append(neighbour_sum(0, PARTS - 1, "x"))
-        a1.append(neighbour_sum(1, PARTS - 1, "y"))
+        a0 = [neighbour_sum(0, b, "x") for b in range(BANKS - 1)]
+        a1 = [neighbour_sum(1, b, "y") for b in range(BANKS - 1)]
+        a0.append(neighbour_sum(0, BANKS - 1, "x"))
+        a1.append(neighbour_sum(1, BANKS - 1, "y"))
 
         wc_w = [keep.tile([P, R], U32, name=f"wc_w{a}", align_bytes=64) for a in range(PASSES)]
         wc_s = [keep.tile([P, R], U8, name=f"wc_s{a}", align_bytes=64) for a in range(PASSES)]
@@ -152,15 +157,11 @@ def tile_list_pnet_gate_kernel(
         wc_bf = [keep.tile([P, PACK * R], BF16, name=f"wc_bf{a}", align_bytes=64)[:] for a in range(PASSES)]
         c_parts = [keep.tile([P, PACK * P], BF16, name=f"c_part{q}", align_bytes=64)[:] for q in range(PARTS)]
 
-        def in_runs(dst, raw):
-            return (
-                dst.rearrange("p (b n i) -> p b i n", n=RUN, i=PACK),
-                raw.rearrange("p i (b n) -> p b i n", n=RUN),
-            )
-
         def round_scalar(dst, raw):
-            dst_runs, raw_runs = in_runs(dst, raw)
-            nc.scalar.copy(out=dst_runs, in_=raw_runs)
+            nc.scalar.copy(
+                out=dst.rearrange("p (b n i) -> p b i n", n=RUN, i=PACK),
+                in_=raw.rearrange("p i (b n) -> p b i n", n=RUN),
+            )
 
         def dealt_runs(dst, raw, lo, hi):
             return (
@@ -176,23 +177,24 @@ def tile_list_pnet_gate_kernel(
         def quantize(words, scales, src):
             nc.vector.quantize_mx(out=words.bitcast(FP8X4), scales=scales, in_=src)
 
-        first = [keep.tile([P, HALF, 2], F32, name=f"first{q}", align_bytes=64) for q in range(PARTS)]
-        for q in range(PARTS):
-            nc.scalar.copy(out=first[q][:], in_=woven(a0[q]))
-        a2 = [neighbour_sum(2, q, "x") for q in range(PARTS)]
+        first = [keep.tile([P, HALF, 2], F32, name=f"first{b}", align_bytes=64) for b in range(BANKS)]
+        for b in range(BANKS):
+            nc.scalar.copy(out=first[b][:], in_=woven(a0[b]))
+        a2 = [neighbour_sum(2, b, "x") for b in range(BANKS)]
 
-        nc.scalar.copy(*dealt_runs(wc_bf[0], wc_raw[0][:], 0, 2))
-        nc.vector.tensor_copy(*dealt_runs(wc_bf[0], wc_raw[0][:], 2, 4))
-        second = keep.tile([P, PARTS, HALF, 2], F32, name="second")
-        for q in range(PARTS):
-            if q == PARTS - 1:
+        nc.scalar.copy(*dealt_runs(wc_bf[0], wc_raw[0][:], 0, PACK // 2))
+        nc.vector.tensor_copy(*dealt_runs(wc_bf[0], wc_raw[0][:], PACK // 2, PACK))
+        second = keep.tile([P, BANKS, HALF, 2], F32, name="second")
+        for b in range(BANKS):
+            if b == BANKS - 1:
                 quantize(wc_w[0][:], wc_s[0][:], wc_bf[0])
-            nc.vector.tensor_tensor(second[:, q], woven(a1[q]), first[q][:], ALU.max)
+            nc.vector.tensor_tensor(second[:, b], woven(a1[b]), first[b][:], ALU.max)
 
         c_bf0 = keep.tile([P, PACK * J], BF16, name="c_bf0", tag="pair", align_bytes=64)
         for q in range(PARTS):
             round_gpsimd(c_bf0[:, PACK * P * q : PACK * P * (q + 1)], c_raw[0][:, :, P * q : P * (q + 1)])
-        nc.scalar.copy(*dealt_runs(wc_bf[1], wc_raw[1][:], 0, 4))
+        nc.scalar.copy(*dealt_runs(wc_bf[1], wc_raw[1][:], 0, PACK))
+
         best = [
             keep.tile([P, 2, HALF, 2], F32, name="best0", align_bytes=64),
             keep.tile([P, 2, HALF, 2], F32, name="best1", tag="wc_bf1", align_bytes=64),
@@ -207,7 +209,7 @@ def tile_list_pnet_gate_kernel(
 
         wd_w = keep.tile([P, N], I32, name="wd_w", tag="pair", align_bytes=64)
         nc.sync.dma_start(out=wd_w[:], in_=wd_words[0].rearrange("p n b -> p (n b)").bitcast(I32))
-        gate = keep.tile([P, N // P, J], F32, name="gate", tag="tab_w", align_bytes=64)
+        gate = relay.tile([P, N // P, J], F32, name="gate", offset=RAW)
         nc.sync.dma_start(out=gate[:], in_=gm.rearrange("(b p) j -> p b j", p=P))
         quantize(wc_w[1][:], wc_s[1][:], wc_bf[1])
 
@@ -256,11 +258,11 @@ def tile_list_pnet_gate_kernel(
             h_s = keep.tile([P, P], U8, name=f"h_s{q}", align_bytes=64)
             quantize(h_w[:], h_s[:], h_parts[q][:])
             bank = psum.tile([P, N // P, P], F32, name=f"y{q}", tag=f"x{q}")
-            for b in range(N // P):
+            for n in range(N // P):
                 nc.tensor.matmul_mx(
-                    out=bank[:, b, :],
-                    lhsT=wd_w[:, P * b : P * (b + 1)].bitcast(FP8X4),
-                    lhsT_scale=planes[:, b, WD_COL:PLANE],
+                    out=bank[:, n, :],
+                    lhsT=wd_w[:, P * n : P * (n + 1)].bitcast(FP8X4),
+                    lhsT_scale=planes[:, n, WD_COL:PLANE],
                     rhs=h_w[:].bitcast(FP8X4),
                     rhs_scale=h_s[:],
                     start=True,

@@ -24,6 +24,7 @@ PARTS = J // P
 HALF = J // 2
 BANKS = 4
 QUADS = 4
+LIVE = 4
 COMPACT = 96
 ROWS = slice(COMPACT, P)
 EARLY = 2
@@ -45,10 +46,10 @@ def tile_list_pnet_gate_kernel(
 
         offsets = keep.tile([P, LISTS * J // 16], U16, name="offsets")
 
-        tab_s = keep.tile([P, T], U8, name="tab_s", tag="tab_s", align_bytes=64)
+        tab_s = keep.tile([P, T], U8, name="tab_s", align_bytes=64)
         planes = keep.tile([P, PASSES, PLANE], U8, name="planes", align_bytes=64)
         planes_late = keep.tile([P, PASSES, J], U8, name="planes_late", align_bytes=64)
-        rows_s = keep.tile([P, PLANE], U8, name="rows_s", tag="rows_s", align_bytes=64)
+        rows_s = relay.tile([P, PLANE], U8, name="rows_s", offset=3 * RAW - J)
         w_rows = keep.tile([P, R], U8, name="w_rows", align_bytes=64)
         nc.vector.memset(tab_s[0:COMPACT, :].bitcast(I32), 0)
         nc.gpsimd.memset(w_rows[0:COMPACT, :].bitcast(I32), 0)
@@ -64,7 +65,7 @@ def tile_list_pnet_gate_kernel(
         )
         tab_w = keep.tile([P, T], I32, name="tab_w", align_bytes=64)
         nc.sync.dma_start(out=tab_w[:], in_=tab_words[0].rearrange("p t b -> p (t b)").bitcast(I32))
-        w_w = keep.tile([P, PASSES, 2 * R], U8, name="w_w", tag="pair", align_bytes=64)
+        w_w = keep.tile([P, PASSES, 2 * R], U8, name="w_w", align_bytes=64)
         nc.sync.dma_start(out=w_w[:].bitcast(I32), in_=w_words.rearrange("a p n -> p a n").bitcast(I32))
 
         nc.vector.tensor_copy(
@@ -80,81 +81,88 @@ def tile_list_pnet_gate_kernel(
         def spread_rows(dst, rows):
             for quad in range(QUADS):
                 nc.sync.dma_start(
-                    out=dst[32 * quad : 32 * quad + 4, :, :].bitcast(I32),
+                    out=dst[32 * quad : 32 * quad + LIVE, :, :].bitcast(I32),
                     in_=rows[COMPACT + 8 * quad : COMPACT + 8 * quad + 8, :].bitcast(I32),
                 )
 
+        def listed(first, count):
+            return offsets[:, first // 16 : (first + count) // 16]
+
         v_rows = [relay.tile([P, J], U8, name=f"v_rows{g}", offset=RAW - J + J * g) for g in range(EARLY)]
         for g in range(EARLY):
-            nc.vector.tensor_copy(v_rows[g][:], tab_s[:].indirect(offsets[:, g * J // 16 : (g + 1) * J // 16]))
+            nc.vector.tensor_copy(v_rows[g][:], tab_s[:].indirect(listed(g * J, J)))
         for g in range(EARLY):
             nc.vector.tensor_copy(rows_s[ROWS, g * J : (g + 1) * J].bitcast(I32), v_rows[g][ROWS, :].bitcast(I32))
         spread_rows(planes, rows_s)
         wc_raw = [load_pass(relay.tile([P, PACK, R], F32, name="wc_raw0", offset=RAW), wc, 0)]
         v_rows_late = relay.tile([P, J], U8, name="v_rows_late", offset=RAW - J)
-        nc.vector.tensor_copy(v_rows_late[:], tab_s[:].indirect(offsets[:, W_COL // 16 :]))
+        nc.vector.tensor_copy(v_rows_late[:], tab_s[:].indirect(listed(EARLY * J, J)))
         spread_rows(planes_late, v_rows_late)
-        c_raw = [load_pass(keep.tile([P, PACK, J], F32, name="c_raw0", tag="tab_s", align_bytes=64), c, 0)]
-        wc_raw.append(load_pass(keep.tile([P, PACK, R], F32, name="wc_raw1", tag="rows_s", align_bytes=64), wc, 1))
+        c_raw = [load_pass(relay.tile([P, PACK, J], F32, name="c_raw0", offset=2 * RAW), c, 0)]
+        wc_raw.append(load_pass(relay.tile([P, PACK, R], F32, name="wc_raw1", offset=3 * RAW), wc, 1))
         c_raw.append(load_pass(relay.tile([P, PACK, J], F32, name="c_raw1", offset=0), c, 1))
-        v_planes = (planes[:, :, 0:J], planes[:, :, J : 2 * J], planes_late[:])
 
-        first_pair = keep.tile([P, J], U32, name="first_pair", align_bytes=64)
-        nc.vector.tensor_copy(first_pair[:], tab_w[:].bitcast(U32).indirect(offsets[:, 0 : J // 16]))
-        halves = first_pair[:].bitcast(U16).rearrange("p (j a) -> p a j", a=PASSES)
+        def v_plane(g, a):
+            return planes[:, a, g * J : (g + 1) * J] if g < EARLY else planes_late[:, a, :]
+
         w_cols = w_w[:].bitcast(U16).rearrange("p a (m t) -> p a t m", t=PACK)
         w_dealt = []
-        v_w = [[]]
-        for n in range(2):
-            w_dealt.append(keep.tile([P, PASSES, R], U8, name=f"w_dealt{n}", align_bytes=64))
-            nc.vector.tensor_copy(
-                w_dealt[n][:].bitcast(U16).rearrange("p a (e m) -> p a e m", e=2), w_cols[:, :, 2 * n : 2 * n + 2, :]
+        for u in range(2):
+            w_dealt.append(keep.tile([P, PASSES, R], U8, name=f"w_dealt{u}", align_bytes=64))
+            nc.scalar.copy(
+                out=w_dealt[u][:].bitcast(U16).rearrange("p a (e m) -> p a e m", e=2),
+                in_=w_cols[:, :, 2 * u : 2 * u + 2, :],
             )
-            v_half = keep.tile([P, PASSES, 2 * HALF], U8, name=f"v_half{n}", align_bytes=64)
-            nc.vector.tensor_copy(v_half[:].bitcast(U16), halves[:, :, HALF * n : HALF * (n + 1)])
-            v_w[0].append(v_half[:])
 
-        late_pair = keep.tile([P, LISTS - 1, J], U32, name="late_pair", tag="pair", align_bytes=64)
-        for g in range(1, LISTS):
-            listed = offsets[:, g * J // 16 : (g + 1) * J // 16]
-            nc.vector.tensor_copy(late_pair[:, g - 1, :], tab_w[:].bitcast(U32).indirect(listed))
-        for g in range(1, LISTS):
-            parted = keep.tile([P, PASSES, 2 * J], U8, name=f"v_late{g}", align_bytes=64)
+        steps = [(g, h) for h in range(2) for g in range(EARLY)] + [(EARLY, h) for h in range(2)]
+        pairs = {}
+        v_w = {}
+
+        def gather(g, h, slot):
+            pairs[g, h] = keep.tile([P, HALF], U32, name=f"pair{g}_{h}", tag=f"pair{slot}", align_bytes=64)
+            nc.vector.tensor_copy(pairs[g, h][:], tab_w[:].bitcast(U32).indirect(listed(g * J + h * HALF, HALF)))
+
+        def part(g, h):
+            v_w[g, h] = keep.tile([P, PASSES, 2 * HALF], U8, name=f"v_w{g}_{h}", tag=f"v_w{g}_{h}", align_bytes=64)
             nc.vector.tensor_copy(
-                parted[:].bitcast(U16), late_pair[:, g - 1, :].bitcast(U16).rearrange("p (j a) -> p a j", a=PASSES)
+                v_w[g, h][:].bitcast(U16), pairs[g, h][:].bitcast(U16).rearrange("p (j a) -> p a j", a=PASSES)
             )
-            v_w.append([parted[:, :, 2 * HALF * h : 2 * HALF * (h + 1)] for h in range(2)])
+
+        for n in range(0, len(steps), 2):
+            for slot in range(2):
+                gather(*steps[n + slot], slot)
+            for slot in range(2):
+                part(*steps[n + slot])
 
         def neighbour_sum(g, b, tag):
             h, u = divmod(b, 2)
             bank = psum.tile([P, 2, HALF], F32, name=f"a{g}_{b}", tag=f"{tag}{b}")
-            for e in range(2):
-                t = 2 * u + e
-                for a in range(PASSES):
+            for a in range(PASSES):
+                for e in range(2):
+                    t = 2 * u + e
                     nc.tensor.matmul_mx(
                         out=bank[:, e, :],
                         lhsT=w_dealt[u][:, a, 2 * P * e : 2 * P * (e + 1)].bitcast(FP4X4),
                         lhsT_scale=planes[:, a, W_COL + P * t : W_COL + P * (t + 1)],
-                        rhs=v_w[g][h][:, a, :].bitcast(FP4X4),
-                        rhs_scale=v_planes[g][:, a, HALF * h : HALF * (h + 1)],
-                        start=(a == 0),
-                        stop=(a == PASSES - 1),
+                        rhs=v_w[g, h][:, a, :].bitcast(FP4X4),
+                        rhs_scale=v_plane(g, a)[:, HALF * h : HALF * (h + 1)],
+                        start=(a == 0 and e == 0),
+                        stop=(a == PASSES - 1 and e == 1),
                     )
             return bank
 
         def woven(bank):
             return bank[:].rearrange("p e j -> p j e")
 
-        a0 = [neighbour_sum(0, b, "x") for b in range(BANKS - 1)]
-        a1 = [neighbour_sum(1, b, "y") for b in range(BANKS - 1)]
-        a0.append(neighbour_sum(0, BANKS - 1, "x"))
-        a1.append(neighbour_sum(1, BANKS - 1, "y"))
+        a0, a1 = [], []
+        for h in range(2):
+            a0.extend(neighbour_sum(0, b, "x") for b in (2 * h, 2 * h + 1))
+            a1.extend(neighbour_sum(1, b, "y") for b in (2 * h, 2 * h + 1))
 
         wc_w = [keep.tile([P, R], U32, name=f"wc_w{a}", align_bytes=64) for a in range(PASSES)]
         wc_s = [keep.tile([P, R], U8, name=f"wc_s{a}", align_bytes=64) for a in range(PASSES)]
         c_w = [keep.tile([P, J], U32, name=f"c_w{a}", align_bytes=64) for a in range(PASSES)]
         c_s = [keep.tile([P, J], U8, name=f"c_s{a}", align_bytes=64) for a in range(PASSES)]
-        wc_bf = [keep.tile([P, PACK * R], BF16, name=f"wc_bf{a}", align_bytes=64)[:] for a in range(PASSES)]
         c_parts = [keep.tile([P, PACK * P], BF16, name=f"c_part{q}", align_bytes=64)[:] for q in range(PARTS)]
 
         def round_scalar(dst, raw):
@@ -182,15 +190,16 @@ def tile_list_pnet_gate_kernel(
             nc.scalar.copy(out=first[b][:], in_=woven(a0[b]))
         a2 = [neighbour_sum(2, b, "x") for b in range(BANKS)]
 
+        wc_bf = [keep.tile([P, PACK * R], BF16, name=f"wc_bf{a}", align_bytes=64)[:] for a in range(PASSES)]
         nc.scalar.copy(*dealt_runs(wc_bf[0], wc_raw[0][:], 0, PACK // 2))
         nc.vector.tensor_copy(*dealt_runs(wc_bf[0], wc_raw[0][:], PACK // 2, PACK))
-        second = keep.tile([P, BANKS, HALF, 2], F32, name="second")
+        second = [keep.tile([P, HALF, 2], F32, name=f"second{b}", align_bytes=64) for b in range(BANKS)]
         for b in range(BANKS):
-            if b == BANKS - 1:
+            if b == BANKS // 2:
                 quantize(wc_w[0][:], wc_s[0][:], wc_bf[0])
-            nc.vector.tensor_tensor(second[:, b], woven(a1[b]), first[b][:], ALU.max)
+            nc.vector.tensor_tensor(second[b][:], woven(a1[b]), first[b][:], ALU.max)
 
-        c_bf0 = keep.tile([P, PACK * J], BF16, name="c_bf0", tag="pair", align_bytes=64)
+        c_bf0 = keep.tile([P, PACK * J], BF16, name="c_bf0", tag="pair1", align_bytes=64)
         for q in range(PARTS):
             round_gpsimd(c_bf0[:, PACK * P * q : PACK * P * (q + 1)], c_raw[0][:, :, P * q : P * (q + 1)])
         nc.scalar.copy(*dealt_runs(wc_bf[1], wc_raw[1][:], 0, PACK))
@@ -201,13 +210,13 @@ def tile_list_pnet_gate_kernel(
         ]
 
         def second_max(b):
-            nc.vector.tensor_tensor(best[b // 2][:, b % 2], woven(a2[b]), second[:, b], ALU.max)
+            nc.vector.tensor_tensor(best[b // 2][:, b % 2], woven(a2[b]), second[b][:], ALU.max)
 
         second_max(0)
         second_max(1)
         quantize(c_w[0][:], c_s[0][:], c_bf0[:])
 
-        wd_w = keep.tile([P, N], I32, name="wd_w", tag="pair", align_bytes=64)
+        wd_w = relay.tile([P, N], I32, name="wd_w", offset=RAW + RAW // 2, align_bytes=64)
         nc.sync.dma_start(out=wd_w[:], in_=wd_words[0].rearrange("p n b -> p (n b)").bitcast(I32))
         gate = relay.tile([P, N // P, J], F32, name="gate", offset=RAW)
         nc.sync.dma_start(out=gate[:], in_=gm.rearrange("(b p) j -> p b j", p=P))

@@ -46,10 +46,10 @@ def tile_list_pnet_gate_kernel(
 
         offsets = keep.tile([P, LISTS * J // 16], U16, name="offsets")
 
-        tab_s = keep.tile([P, T], U8, name="tab_s", align_bytes=64)
+        tab_s = relay.tile([P, T], U8, name="tab_s", offset=4 * RAW - T // 2)
         planes = keep.tile([P, PASSES, PLANE], U8, name="planes", align_bytes=64)
         planes_late = keep.tile([P, PASSES, J], U8, name="planes_late", align_bytes=64)
-        rows_s = relay.tile([P, PLANE], U8, name="rows_s", offset=3 * RAW - J)
+        rows_s = relay.tile([P, PLANE], U8, name="rows_s", offset=5 * RAW)
         w_rows = keep.tile([P, R], U8, name="w_rows", align_bytes=64)
         nc.vector.memset(tab_s[0:COMPACT, :].bitcast(I32), 0)
         nc.gpsimd.memset(w_rows[0:COMPACT, :].bitcast(I32), 0)
@@ -98,9 +98,9 @@ def tile_list_pnet_gate_kernel(
         v_rows_late = relay.tile([P, J], U8, name="v_rows_late", offset=RAW - J)
         nc.vector.tensor_copy(v_rows_late[:], tab_s[:].indirect(listed(EARLY * J, J)))
         spread_rows(planes_late, v_rows_late)
-        c_raw = [load_pass(relay.tile([P, PACK, J], F32, name="c_raw0", offset=2 * RAW), c, 0)]
-        wc_raw.append(load_pass(relay.tile([P, PACK, R], F32, name="wc_raw1", offset=3 * RAW), wc, 1))
-        c_raw.append(load_pass(relay.tile([P, PACK, J], F32, name="c_raw1", offset=0), c, 1))
+        c_raw = [load_pass(relay.tile([P, PACK, J], F32, name="c_raw0", offset=3 * RAW), c, 0)]
+        wc_raw.append(load_pass(relay.tile([P, PACK, R], F32, name="wc_raw1", offset=4 * RAW), wc, 1))
+        c_raw.append(load_pass(relay.tile([P, PACK, J], F32, name="c_raw1", offset=5 * RAW), c, 1))
 
         def v_plane(g, a):
             return planes[:, a, g * J : (g + 1) * J] if g < EARLY else planes_late[:, a, :]
@@ -154,14 +154,9 @@ def tile_list_pnet_gate_kernel(
         def woven(bank):
             return bank[:].rearrange("p e j -> p j e")
 
-        a0, a1 = [], []
-        for h in range(2):
-            a0.extend(neighbour_sum(0, b, "x") for b in (2 * h, 2 * h + 1))
-            a1.extend(neighbour_sum(1, b, "y") for b in (2 * h, 2 * h + 1))
-
-        wc_w = [keep.tile([P, R], U32, name=f"wc_w{a}", align_bytes=64) for a in range(PASSES)]
+        wc_w = [keep.tile([P, R], U32, name="wc_w0", align_bytes=64)]
         wc_s = [keep.tile([P, R], U8, name=f"wc_s{a}", align_bytes=64) for a in range(PASSES)]
-        c_w = [keep.tile([P, J], U32, name=f"c_w{a}", align_bytes=64) for a in range(PASSES)]
+        c_w = [keep.tile([P, J], U32, name="c_w0", align_bytes=64)]
         c_s = [keep.tile([P, J], U8, name=f"c_s{a}", align_bytes=64) for a in range(PASSES)]
         c_parts = [keep.tile([P, PACK * P], BF16, name=f"c_part{q}", align_bytes=64)[:] for q in range(PARTS)]
 
@@ -185,36 +180,41 @@ def tile_list_pnet_gate_kernel(
         def quantize(words, scales, src):
             nc.vector.quantize_mx(out=words.bitcast(FP8X4), scales=scales, in_=src)
 
-        first = [keep.tile([P, HALF, 2], F32, name=f"first{b}", align_bytes=64) for b in range(BANKS)]
+        a0, a1 = [], []
         for b in range(BANKS):
-            nc.scalar.copy(out=first[b][:], in_=woven(a0[b]))
-        a2 = [neighbour_sum(2, b, "x") for b in range(BANKS)]
-
+            a0.append(neighbour_sum(0, b, "x"))
+            a1.append(neighbour_sum(1, b, "y"))
         wc_bf = [keep.tile([P, PACK * R], BF16, name=f"wc_bf{a}", align_bytes=64)[:] for a in range(PASSES)]
         nc.scalar.copy(*dealt_runs(wc_bf[0], wc_raw[0][:], 0, PACK // 2))
         nc.vector.tensor_copy(*dealt_runs(wc_bf[0], wc_raw[0][:], PACK // 2, PACK))
-        second = [keep.tile([P, HALF, 2], F32, name=f"second{b}", align_bytes=64) for b in range(BANKS)]
+        quantize(wc_w[0][:], wc_s[0][:], wc_bf[0])
+        first = [
+            keep.tile([P, HALF, 2], F32, name="first0"),
+            relay.tile([P, HALF, 2], F32, name="first1", offset=RAW + RAW // 4),
+            relay.tile([P, HALF, 2], F32, name="first2", offset=2 * RAW - RAW // 4),
+            relay.tile([P, HALF, 2], F32, name="first3", offset=RAW),
+        ]
+        pooled01 = relay.tile([P, BANKS, HALF, 2], F32, name="second", offset=0)
+        second = [pooled01[:, b] for b in range(BANKS)]
         for b in range(BANKS):
-            if b == BANKS // 2:
-                quantize(wc_w[0][:], wc_s[0][:], wc_bf[0])
-            nc.vector.tensor_tensor(second[b][:], woven(a1[b]), first[b][:], ALU.max)
+            nc.scalar.copy(out=first[b][:], in_=woven(a0[b]))
+            nc.vector.tensor_tensor(second[b], woven(a1[b]), first[b][:], ALU.max)
+        a2 = [neighbour_sum(2, b, "x") for b in range(BANKS)]
+        best = [relay.tile([P, 2, HALF, 2], F32, name="best0", offset=2 * RAW - RAW // 4)]
+
+        def second_max(b):
+            nc.vector.tensor_tensor(best[b // 2][:, b % 2], woven(a2[b]), second[b], ALU.max)
+
+        second_max(0)
+        second_max(1)
 
         c_bf0 = keep.tile([P, PACK * J], BF16, name="c_bf0", tag="pair1", align_bytes=64)
         for q in range(PARTS):
             round_gpsimd(c_bf0[:, PACK * P * q : PACK * P * (q + 1)], c_raw[0][:, :, P * q : P * (q + 1)])
         nc.scalar.copy(*dealt_runs(wc_bf[1], wc_raw[1][:], 0, PACK))
-
-        best = [
-            keep.tile([P, 2, HALF, 2], F32, name="best0", align_bytes=64),
-            keep.tile([P, 2, HALF, 2], F32, name="best1", tag="wc_bf1", align_bytes=64),
-        ]
-
-        def second_max(b):
-            nc.vector.tensor_tensor(best[b // 2][:, b % 2], woven(a2[b]), second[b][:], ALU.max)
-
-        second_max(0)
-        second_max(1)
         quantize(c_w[0][:], c_s[0][:], c_bf0[:])
+        wc_w.append(relay.tile([P, R], U32, name="wc_w1", offset=3 * RAW + RAW // 2, align_bytes=64))
+        c_w.append(relay.tile([P, J], U32, name="c_w1", offset=4 * RAW - RAW // 4, align_bytes=64))
 
         wd_w = relay.tile([P, N], I32, name="wd_w", offset=RAW + RAW // 2, align_bytes=64)
         nc.sync.dma_start(out=wd_w[:], in_=wd_words[0].rearrange("p n b -> p (n b)").bitcast(I32))
@@ -242,6 +242,7 @@ def tile_list_pnet_gate_kernel(
                     )
             own.append(bank)
 
+        best.append(keep.tile([P, 2, HALF, 2], F32, name="best1", tag="wc_bf1", align_bytes=64))
         second_max(2)
         second_max(3)
         out_rows = out.rearrange("(b p) j -> p b j", p=P)

@@ -156,7 +156,7 @@ def tile_list_pnet_gate_kernel(
 
         wc_w = [keep.tile([P, R], U32, name="wc_w0", align_bytes=64)]
         wc_s = [keep.tile([P, R], U8, name=f"wc_s{a}", align_bytes=64) for a in range(PASSES)]
-        c_w = [keep.tile([P, J], U32, name="c_w0", align_bytes=64)]
+        c0_w = [keep.tile([P, HALF], U32, name="c0_w0", align_bytes=64)]
         c_s = [keep.tile([P, J], U8, name=f"c_s{a}", align_bytes=64) for a in range(PASSES)]
         c_parts = [keep.tile([P, PACK * P], BF16, name=f"c_part{q}", align_bytes=64)[:] for q in range(PARTS)]
 
@@ -212,9 +212,12 @@ def tile_list_pnet_gate_kernel(
         for q in range(PARTS):
             round_gpsimd(c_bf0[:, PACK * P * q : PACK * P * (q + 1)], c_raw[0][:, :, P * q : P * (q + 1)])
         nc.scalar.copy(*dealt_runs(wc_bf[1], wc_raw[1][:], 0, PACK))
-        quantize(c_w[0][:], c_s[0][:], c_bf0[:])
+        quantize(c0_w[0][:], c_s[0][:, 0:HALF], c_bf0[:, 0 : PACK * HALF])
+        best.append(relay.tile([P, 2, HALF, 2], F32, name="best1", offset=3 * RAW))
+        second_max(2)
+        second_max(3)
         wc_w.append(relay.tile([P, R], U32, name="wc_w1", offset=3 * RAW + RAW // 2, align_bytes=64))
-        c_w.append(relay.tile([P, J], U32, name="c_w1", offset=4 * RAW - RAW // 4, align_bytes=64))
+        c1_w = relay.tile([P, J], U32, name="c1_w", offset=4 * RAW - RAW // 4, align_bytes=64)
 
         wd_w = relay.tile([P, N], I32, name="wd_w", offset=RAW + RAW // 2, align_bytes=64)
         nc.sync.dma_start(out=wd_w[:], in_=wd_words[0].rearrange("p n b -> p (n b)").bitcast(I32))
@@ -227,7 +230,11 @@ def tile_list_pnet_gate_kernel(
         own = []
         for q in range(PARTS):
             cols = slice(q * P, (q + 1) * P)
-            quantize(c_w[1][:, cols], c_s[1][:, cols], c_parts[q])
+            quantize(c1_w[:, cols], c_s[1][:, cols], c_parts[q])
+            if q == 0:
+                c0_w.append(keep.tile([P, HALF], U32, name="c0_w1", tag="c_part0", align_bytes=64))
+                quantize(c0_w[1][:], c_s[0][:, HALF:J], c_bf0[:, PACK * HALF : PACK * J])
+            c_words = (c0_w[q // 2][:, P * (q % 2) : P * (q % 2 + 1)], c1_w[:, cols])
             bank = psum.tile([P, PACK, P], F32, name=f"own{q}", tag=f"y{q}")
             for a in range(PASSES):
                 for t in range(PACK):
@@ -235,16 +242,13 @@ def tile_list_pnet_gate_kernel(
                         out=bank[:, t, :],
                         lhsT=wc_w[a][:, P * t : P * (t + 1)].bitcast(FP8X4),
                         lhsT_scale=wc_s[a][:, P * t : P * (t + 1)],
-                        rhs=c_w[a][:, cols].bitcast(FP8X4),
+                        rhs=c_words[a].bitcast(FP8X4),
                         rhs_scale=c_s[a][:, cols],
                         start=(a == 0 and t == 0),
                         stop=(a == PASSES - 1 and t == PACK - 1),
                     )
             own.append(bank)
 
-        best.append(keep.tile([P, 2, HALF, 2], F32, name="best1", tag="wc_bf1", align_bytes=64))
-        second_max(2)
-        second_max(3)
         out_rows = out.rearrange("(b p) j -> p b j", p=P)
         h_parts = []
         for q in range(PARTS):

@@ -33,6 +33,9 @@ WD_COL = W_COL + R
 PLANE = WD_COL + P
 RAW = PACK * J * 4
 RUN = 4
+COPY = HALF * 2 * 4
+
+AT_SECOND, AT_WC0, AT_C0, AT_WC1, AT_C1 = 0, RAW, 3 * RAW, 4 * RAW, 5 * RAW
 
 
 def tile_list_pnet_gate_kernel(
@@ -46,10 +49,10 @@ def tile_list_pnet_gate_kernel(
 
         offsets = keep.tile([P, LISTS * J // 16], U16, name="offsets")
 
-        tab_s = relay.tile([P, T], U8, name="tab_s", offset=4 * RAW - T // 2)
+        tab_s = relay.tile([P, T], U8, name="tab_s", offset=AT_WC1 - T // 2)
         planes = keep.tile([P, PASSES, PLANE], U8, name="planes", align_bytes=64)
         planes_late = keep.tile([P, PASSES, J], U8, name="planes_late", align_bytes=64)
-        rows_s = relay.tile([P, PLANE], U8, name="rows_s", offset=5 * RAW)
+        rows_s = relay.tile([P, PLANE], U8, name="rows_s", offset=AT_C1)
         w_rows = keep.tile([P, R], U8, name="w_rows", align_bytes=64)
         nc.vector.memset(tab_s[0:COMPACT, :].bitcast(I32), 0)
         nc.gpsimd.memset(w_rows[0:COMPACT, :].bitcast(I32), 0)
@@ -85,22 +88,22 @@ def tile_list_pnet_gate_kernel(
                     in_=rows[COMPACT + 8 * quad : COMPACT + 8 * quad + 8, :].bitcast(I32),
                 )
 
-        def listed(first, count):
-            return offsets[:, first // 16 : (first + count) // 16]
+        def listed(entry, count):
+            return offsets[:, entry // 16 : (entry + count) // 16]
 
-        v_rows = [relay.tile([P, J], U8, name=f"v_rows{g}", offset=RAW - J + J * g) for g in range(EARLY)]
+        v_rows = [relay.tile([P, J], U8, name=f"v_rows{g}", offset=AT_WC0 - J + J * g) for g in range(EARLY)]
         for g in range(EARLY):
             nc.vector.tensor_copy(v_rows[g][:], tab_s[:].indirect(listed(g * J, J)))
         for g in range(EARLY):
             nc.vector.tensor_copy(rows_s[ROWS, g * J : (g + 1) * J].bitcast(I32), v_rows[g][ROWS, :].bitcast(I32))
         spread_rows(planes, rows_s)
-        wc_raw = [load_pass(relay.tile([P, PACK, R], F32, name="wc_raw0", offset=RAW), wc, 0)]
-        v_rows_late = relay.tile([P, J], U8, name="v_rows_late", offset=RAW - J)
+        wc_raw = [load_pass(relay.tile([P, PACK, R], F32, name="wc_raw0", offset=AT_WC0), wc, 0)]
+        v_rows_late = relay.tile([P, J], U8, name="v_rows_late", offset=AT_WC0 - J)
         nc.vector.tensor_copy(v_rows_late[:], tab_s[:].indirect(listed(EARLY * J, J)))
         spread_rows(planes_late, v_rows_late)
-        c_raw = [load_pass(relay.tile([P, PACK, J], F32, name="c_raw0", offset=3 * RAW), c, 0)]
-        wc_raw.append(load_pass(relay.tile([P, PACK, R], F32, name="wc_raw1", offset=4 * RAW), wc, 1))
-        c_raw.append(load_pass(relay.tile([P, PACK, J], F32, name="c_raw1", offset=5 * RAW), c, 1))
+        c_raw = [load_pass(relay.tile([P, PACK, J], F32, name="c_raw0", offset=AT_C0), c, 0)]
+        wc_raw.append(load_pass(relay.tile([P, PACK, R], F32, name="wc_raw1", offset=AT_WC1), wc, 1))
+        c_raw.append(load_pass(relay.tile([P, PACK, J], F32, name="c_raw1", offset=AT_C1), c, 1))
 
         def v_plane(g, a):
             return planes[:, a, g * J : (g + 1) * J] if g < EARLY else planes_late[:, a, :]
@@ -123,7 +126,7 @@ def tile_list_pnet_gate_kernel(
             nc.vector.tensor_copy(pairs[g, h][:], tab_w[:].bitcast(U32).indirect(listed(g * J + h * HALF, HALF)))
 
         def part(g, h):
-            v_w[g, h] = keep.tile([P, PASSES, 2 * HALF], U8, name=f"v_w{g}_{h}", tag=f"v_w{g}_{h}", align_bytes=64)
+            v_w[g, h] = keep.tile([P, PASSES, 2 * HALF], U8, name=f"v_w{g}_{h}", align_bytes=64)
             nc.vector.tensor_copy(
                 v_w[g, h][:].bitcast(U16), pairs[g, h][:].bitcast(U16).rearrange("p (j a) -> p a j", a=PASSES)
             )
@@ -184,26 +187,28 @@ def tile_list_pnet_gate_kernel(
         for b in range(BANKS):
             a0.append(neighbour_sum(0, b, "x"))
             a1.append(neighbour_sum(1, b, "y"))
+
         wc_bf = [keep.tile([P, PACK * R], BF16, name=f"wc_bf{a}", align_bytes=64)[:] for a in range(PASSES)]
         nc.scalar.copy(*dealt_runs(wc_bf[0], wc_raw[0][:], 0, PACK // 2))
         nc.vector.tensor_copy(*dealt_runs(wc_bf[0], wc_raw[0][:], PACK // 2, PACK))
         quantize(wc_w[0][:], wc_s[0][:], wc_bf[0])
+
         first = [
             keep.tile([P, HALF, 2], F32, name="first0"),
-            relay.tile([P, HALF, 2], F32, name="first1", offset=RAW + RAW // 4),
-            relay.tile([P, HALF, 2], F32, name="first2", offset=2 * RAW - RAW // 4),
-            relay.tile([P, HALF, 2], F32, name="first3", offset=RAW),
+            relay.tile([P, HALF, 2], F32, name="first1", offset=AT_WC0 + COPY),
+            relay.tile([P, HALF, 2], F32, name="first2", offset=AT_WC0 + RAW - COPY),
+            relay.tile([P, HALF, 2], F32, name="first3", offset=AT_WC0),
         ]
-        pooled01 = relay.tile([P, BANKS, HALF, 2], F32, name="second", offset=0)
-        second = [pooled01[:, b] for b in range(BANKS)]
+        second = relay.tile([P, BANKS, HALF, 2], F32, name="second", offset=AT_SECOND)
         for b in range(BANKS):
             nc.scalar.copy(out=first[b][:], in_=woven(a0[b]))
-            nc.vector.tensor_tensor(second[b], woven(a1[b]), first[b][:], ALU.max)
+            nc.vector.tensor_tensor(second[:, b], woven(a1[b]), first[b][:], ALU.max)
         a2 = [neighbour_sum(2, b, "x") for b in range(BANKS)]
-        best = [relay.tile([P, 2, HALF, 2], F32, name="best0", offset=2 * RAW - RAW // 4)]
+
+        best = [relay.tile([P, 2, HALF, 2], F32, name="best0", offset=AT_WC0 + RAW - COPY)]
 
         def second_max(b):
-            nc.vector.tensor_tensor(best[b // 2][:, b % 2], woven(a2[b]), second[b], ALU.max)
+            nc.vector.tensor_tensor(best[b // 2][:, b % 2], woven(a2[b]), second[:, b], ALU.max)
 
         second_max(0)
         second_max(1)
@@ -212,16 +217,17 @@ def tile_list_pnet_gate_kernel(
         for q in range(PARTS):
             round_gpsimd(c_bf0[:, PACK * P * q : PACK * P * (q + 1)], c_raw[0][:, :, P * q : P * (q + 1)])
         nc.scalar.copy(*dealt_runs(wc_bf[1], wc_raw[1][:], 0, PACK))
+
         quantize(c0_w[0][:], c_s[0][:, 0:HALF], c_bf0[:, 0 : PACK * HALF])
-        best.append(relay.tile([P, 2, HALF, 2], F32, name="best1", offset=3 * RAW))
+        best.append(relay.tile([P, 2, HALF, 2], F32, name="best1", offset=AT_C0))
         second_max(2)
         second_max(3)
-        wc_w.append(relay.tile([P, R], U32, name="wc_w1", offset=3 * RAW + RAW // 2, align_bytes=64))
-        c1_w = relay.tile([P, J], U32, name="c1_w", offset=4 * RAW - RAW // 4, align_bytes=64)
+        wc_w.append(relay.tile([P, R], U32, name="wc_w1", offset=AT_C0 + 2 * COPY, align_bytes=64))
+        c1_w = relay.tile([P, J], U32, name="c1_w", offset=AT_C0 + 3 * COPY, align_bytes=64)
 
-        wd_w = relay.tile([P, N], I32, name="wd_w", offset=RAW + RAW // 2, align_bytes=64)
+        wd_w = relay.tile([P, N], I32, name="wd_w", offset=AT_WC0 + 2 * COPY, align_bytes=64)
         nc.sync.dma_start(out=wd_w[:], in_=wd_words[0].rearrange("p n b -> p (n b)").bitcast(I32))
-        gate = relay.tile([P, N // P, J], F32, name="gate", offset=RAW)
+        gate = relay.tile([P, N // P, J], F32, name="gate", offset=AT_WC0)
         nc.sync.dma_start(out=gate[:], in_=gm.rearrange("(b p) j -> p b j", p=P))
         quantize(wc_w[1][:], wc_s[1][:], wc_bf[1])
 
@@ -252,7 +258,7 @@ def tile_list_pnet_gate_kernel(
         out_rows = out.rearrange("(b p) j -> p b j", p=P)
         h_parts = []
         for q in range(PARTS):
-            summed = keep.tile([P, PACK * P], BF16, name=f"summed{q}")
+            summed = keep.tile([P, PACK * P], BF16, name=f"summed{q}", tag=f"summed{q}")
             pooled = best[q // 2][:, :, P * (q % 2) : P * (q % 2 + 1), :]
             nc.vector.tensor_tensor(
                 summed[:].rearrange("p (j u e) -> p j u e", u=2, e=2),
@@ -284,14 +290,14 @@ def tile_list_pnet_gate_kernel(
                 )
             return bank
 
+        late = keep.tile([P, PARTS - 1, N // P, P], F32, name="late_results", tag=f"summed{PARTS - 1}")
+
         def gate_and_store(q, bank):
             cols = slice(q * P, (q + 1) * P)
-            res = keep.tile([P, N // P, P], F32, name=f"res{q}")
-            nc.vector.tensor_tensor(res[:], bank[:], gate[:, :, cols], ALU.mult)
-            nc.sync.dma_start(out=out_rows[:, :, cols], in_=res[:])
+            res = keep.tile([P, N // P, P], F32, name="res0")[:] if q == 0 else late[:, q - 1]
+            nc.vector.tensor_tensor(res, bank[:], gate[:, :, cols], ALU.mult)
+            nc.sync.dma_start(out=out_rows[:, :, cols], in_=res)
 
-        y = [second_layer(0)]
-        for q in range(1, PARTS):
-            y.append(second_layer(q))
-            gate_and_store(q - 1, y[q - 1])
-        gate_and_store(PARTS - 1, y[PARTS - 1])
+        y = [second_layer(q) for q in range(PARTS)]
+        for q in range(PARTS):
+            gate_and_store(q, y[q])

from contextlib import ExitStack

import concourse.mybir as mybir

K, R, N, T, J = 1024, 512, 256, 4096, 512
LISTS = 3
FLOPS = 2 * (LISTS + 1) * K * R * J + 2 * R * N * J

F32 = mybir.dt.float32
BF16 = mybir.dt.bfloat16
I32 = mybir.dt.int32
U32 = mybir.dt.uint32
U16 = mybir.dt.uint16
U8 = mybir.dt.uint8
FP8X4 = mybir.dt.float8_e4m3fn_x4
FP4X4 = mybir.dt.float4_e2m1fn_x4
ALU = mybir.AluOpType
ACT = mybir.ActivationFunctionType

P = 128
PACK = 4
PASSES = K // (P * PACK)
PARTS = J // P
HALF = J // 2
BANKS = 4
QUADS = 4
LIVE = 4
COMPACT = 96
ROWS = slice(COMPACT, P)
EARLY = 2
W_COL = EARLY * J
WD_COL = W_COL + R
PLANE = WD_COL + P
RAW = PACK * J * 4
RUN = 4
COPY = HALF * 2 * 4

AT_SECOND, AT_WC0, AT_C0, AT_WC1, AT_C1 = 0, RAW, 3 * RAW, 4 * RAW, 5 * RAW


def tile_list_pnet_gate_kernel(
    tc, tab_words, tab_scales, c, w_words, w_scales, wc, wd_words, wd_scales, gm, offs, out
):
    nc = tc.nc
    with ExitStack() as ctx:
        keep = ctx.enter_context(tc.tile_pool(name="keep", bufs=1))
        relay = ctx.enter_context(tc.tile_pool(name="relay", bufs=1))
        psum = ctx.enter_context(tc.psum_pool(name="psum", bufs=1))

        offsets = keep.tile([P, LISTS * J // 16], U16, name="offsets")

        tab_s = relay.tile([P, T], U8, name="tab_s", offset=AT_WC1 - T // 2)
        planes = keep.tile([P, PASSES, PLANE], U8, name="planes", align_bytes=64)
        planes_late = keep.tile([P, PASSES, J], U8, name="planes_late", align_bytes=64)
        rows_s = relay.tile([P, PLANE], U8, name="rows_s", offset=AT_C1)
        w_rows = keep.tile([P, R], U8, name="w_rows", align_bytes=64)
        nc.vector.memset(tab_s[0:COMPACT, :].bitcast(I32), 0)
        nc.gpsimd.memset(w_rows[0:COMPACT, :].bitcast(I32), 0)
        nc.gpsimd.memset(planes[:].bitcast(I32), 0)
        nc.gpsimd.memset(planes_late[:].bitcast(I32), 0)

        nc.sync.dma_start(out=w_rows[ROWS, :].bitcast(I32), in_=w_scales.rearrange("a s r -> s a r").bitcast(I32))
        nc.sync.dma_start(offsets[:], offs)
        nc.scalar.dma_start(out=tab_s[ROWS, :].bitcast(I32), in_=tab_scales.rearrange("a s t -> s a t").bitcast(I32))
        nc.scalar.dma_start(
            out=rows_s[ROWS, WD_COL:PLANE].bitcast(I32),
            in_=wd_scales[0].rearrange("s (b n) -> (s b) n", n=P).bitcast(I32),
        )
        tab_w = keep.tile([P, T], I32, name="tab_w", align_bytes=64)
        nc.sync.dma_start(out=tab_w[:], in_=tab_words[0].rearrange("p t b -> p (t b)").bitcast(I32))
        w_w = keep.tile([P, PASSES, 2 * R], U8, name="w_w", align_bytes=64)
        nc.sync.dma_start(out=w_w[:].bitcast(I32), in_=w_words.rearrange("a p n -> p a n").bitcast(I32))

        nc.vector.tensor_copy(
            rows_s[:, W_COL:WD_COL].rearrange("p (t m) -> p t m", t=PACK),
            w_rows[:].rearrange("p (m t) -> p t m", t=PACK),
        )

        def load_pass(raw, src, a):
            rows = src[a * P * PACK : (a + 1) * P * PACK, :]
            nc.sync.dma_start(out=raw[:], in_=rows.rearrange("(p i) n -> p i n", i=PACK))
            return raw

        def spread_rows(dst, rows):
            for quad in range(QUADS):
                nc.sync.dma_start(
                    out=dst[32 * quad : 32 * quad + LIVE, :, :].bitcast(I32),
                    in_=rows[COMPACT + 8 * quad : COMPACT + 8 * quad + 8, :].bitcast(I32),
                )

        def listed(entry, count):
            return offsets[:, entry // 16 : (entry + count) // 16]

        v_rows = [relay.tile([P, J], U8, name=f"v_rows{g}", offset=AT_WC0 - J + J * g) for g in range(EARLY)]
        for g in range(EARLY):
            nc.vector.tensor_copy(v_rows[g][:], tab_s[:].indirect(listed(g * J, J)))
        for g in range(EARLY):
            nc.vector.tensor_copy(rows_s[ROWS, g * J : (g + 1) * J].bitcast(I32), v_rows[g][ROWS, :].bitcast(I32))
        spread_rows(planes, rows_s)
        wc_raw = [load_pass(relay.tile([P, PACK, R], F32, name="wc_raw0", offset=AT_WC0), wc, 0)]
        v_rows_late = relay.tile([P, J], U8, name="v_rows_late", offset=AT_WC0 - J)
        nc.vector.tensor_copy(v_rows_late[:], tab_s[:].indirect(listed(EARLY * J, J)))
        spread_rows(planes_late, v_rows_late)
        c_raw = [load_pass(relay.tile([P, PACK, J], F32, name="c_raw0", offset=AT_C0), c, 0)]
        wc_raw.append(load_pass(relay.tile([P, PACK, R], F32, name="wc_raw1", offset=AT_WC1), wc, 1))
        c_raw.append(load_pass(relay.tile([P, PACK, J], F32, name="c_raw1", offset=AT_C1), c, 1))

        def v_plane(g, a):
            return planes[:, a, g * J : (g + 1) * J] if g < EARLY else planes_late[:, a, :]

        w_cols = w_w[:].bitcast(U16).rearrange("p a (m t) -> p a t m", t=PACK)
        w_dealt = []
        for u in range(2):
            w_dealt.append(keep.tile([P, PASSES, R], U8, name=f"w_dealt{u}", align_bytes=64))
            nc.scalar.copy(
                out=w_dealt[u][:].bitcast(U16).rearrange("p a (e m) -> p a e m", e=2),
                in_=w_cols[:, :, 2 * u : 2 * u + 2, :],
            )

        steps = [(g, h) for h in range(2) for g in range(EARLY)] + [(EARLY, h) for h in range(2)]
        pairs = {}
        v_w = {}

        def gather(g, h, slot):
            pairs[g, h] = keep.tile([P, HALF], U32, name=f"pair{g}_{h}", tag=f"pair{slot}", align_bytes=64)
            nc.vector.tensor_copy(pairs[g, h][:], tab_w[:].bitcast(U32).indirect(listed(g * J + h * HALF, HALF)))

        def part(g, h):
            v_w[g, h] = keep.tile([P, PASSES, 2 * HALF], U8, name=f"v_w{g}_{h}", align_bytes=64)
            nc.vector.tensor_copy(
                v_w[g, h][:].bitcast(U16), pairs[g, h][:].bitcast(U16).rearrange("p (j a) -> p a j", a=PASSES)
            )

        for n in range(0, len(steps), 2):
            for slot in range(2):
                gather(*steps[n + slot], slot)
            for slot in range(2):
                part(*steps[n + slot])

        def neighbour_sum(g, b, tag):
            h, u = divmod(b, 2)
            bank = psum.tile([P, 2, HALF], F32, name=f"a{g}_{b}", tag=f"{tag}{b}")
            for a in range(PASSES):
                for e in range(2):
                    t = 2 * u + e
                    nc.tensor.matmul_mx(
                        out=bank[:, e, :],
                        lhsT=w_dealt[u][:, a, 2 * P * e : 2 * P * (e + 1)].bitcast(FP4X4),
                        lhsT_scale=planes[:, a, W_COL + P * t : W_COL + P * (t + 1)],
                        rhs=v_w[g, h][:, a, :].bitcast(FP4X4),
                        rhs_scale=v_plane(g, a)[:, HALF * h : HALF * (h + 1)],
                        start=(a == 0 and e == 0),
                        stop=(a == PASSES - 1 and e == 1),
                    )
            return bank

        def woven(bank):
            return bank[:].rearrange("p e j -> p j e")

        wc_w = [keep.tile([P, R], U32, name="wc_w0", align_bytes=64)]
        wc_s = [keep.tile([P, R], U8, name=f"wc_s{a}", align_bytes=64) for a in range(PASSES)]
        c0_w = [keep.tile([P, HALF], U32, name="c0_w0", align_bytes=64)]
        c_s = [keep.tile([P, J], U8, name=f"c_s{a}", align_bytes=64) for a in range(PASSES)]
        c_parts = [keep.tile([P, PACK * P], BF16, name=f"c_part{q}", align_bytes=64)[:] for q in range(PARTS)]

        def round_scalar(dst, raw):
            nc.scalar.copy(
                out=dst.rearrange("p (b n i) -> p b i n", n=RUN, i=PACK),
                in_=raw.rearrange("p i (b n) -> p b i n", n=RUN),
            )

        def dealt_runs(dst, raw, lo, hi):
            return (
                dst[:, PACK * P * lo : PACK * P * hi].rearrange("p (t m i) -> p m i t", m=P, i=PACK),
                raw.rearrange("p i (m t) -> p m i t", t=PACK)[:, :, :, lo:hi],
            )

        def round_gpsimd(dst, raw):
            nc.gpsimd.tensor_scalar(
                dst.rearrange("p (n i) -> p n i", i=PACK), raw.rearrange("p i n -> p n i"), 1.0, 0.0, ALU.mult, ALU.add
            )

        def quantize(words, scales, src):
            nc.vector.quantize_mx(out=words.bitcast(FP8X4), scales=scales, in_=src)

        a0, a1 = [], []
        for b in range(BANKS):
            a0.append(neighbour_sum(0, b, "x"))
            a1.append(neighbour_sum(1, b, "y"))

        wc_bf = [keep.tile([P, PACK * R], BF16, name=f"wc_bf{a}", align_bytes=64)[:] for a in range(PASSES)]
        nc.scalar.copy(*dealt_runs(wc_bf[0], wc_raw[0][:], 0, PACK // 2))
        nc.vector.tensor_copy(*dealt_runs(wc_bf[0], wc_raw[0][:], PACK // 2, PACK))
        quantize(wc_w[0][:], wc_s[0][:], wc_bf[0])

        first = [
            keep.tile([P, HALF, 2], F32, name="first0"),
            relay.tile([P, HALF, 2], F32, name="first1", offset=AT_WC0 + COPY),
            relay.tile([P, HALF, 2], F32, name="first2", offset=AT_WC0 + RAW - COPY),
            relay.tile([P, HALF, 2], F32, name="first3", offset=AT_WC0),
        ]
        second = relay.tile([P, BANKS, HALF, 2], F32, name="second", offset=AT_SECOND)
        for b in range(BANKS):
            nc.scalar.copy(out=first[b][:], in_=woven(a0[b]))
            nc.vector.tensor_tensor(second[:, b], woven(a1[b]), first[b][:], ALU.max)
        a2 = [neighbour_sum(2, b, "x") for b in range(BANKS)]

        best = [relay.tile([P, 2, HALF, 2], F32, name="best0", offset=AT_WC0 + RAW - COPY)]

        def second_max(b):
            nc.vector.tensor_tensor(best[b // 2][:, b % 2], woven(a2[b]), second[:, b], ALU.max)

        second_max(0)
        second_max(1)

        c_bf0 = keep.tile([P, PACK * J], BF16, name="c_bf0", tag="pair1", align_bytes=64)
        for q in range(PARTS):
            round_gpsimd(c_bf0[:, PACK * P * q : PACK * P * (q + 1)], c_raw[0][:, :, P * q : P * (q + 1)])
        nc.scalar.copy(*dealt_runs(wc_bf[1], wc_raw[1][:], 0, PACK))

        quantize(c0_w[0][:], c_s[0][:, 0:HALF], c_bf0[:, 0 : PACK * HALF])
        best.append(relay.tile([P, 2, HALF, 2], F32, name="best1", offset=AT_C0))
        second_max(2)
        second_max(3)
        wc_w.append(relay.tile([P, R], U32, name="wc_w1", offset=AT_C0 + 2 * COPY, align_bytes=64))
        c1_w = relay.tile([P, J], U32, name="c1_w", offset=AT_C0 + 3 * COPY, align_bytes=64)

        wd_w = relay.tile([P, N], I32, name="wd_w", offset=AT_WC0 + 2 * COPY, align_bytes=64)
        nc.sync.dma_start(out=wd_w[:], in_=wd_words[0].rearrange("p n b -> p (n b)").bitcast(I32))
        gate = relay.tile([P, N // P, J], F32, name="gate", offset=AT_WC0)
        nc.sync.dma_start(out=gate[:], in_=gm.rearrange("(b p) j -> p b j", p=P))
        quantize(wc_w[1][:], wc_s[1][:], wc_bf[1])

        for q in range(PARTS):
            round_scalar(c_parts[q], c_raw[1][:, :, q * P : (q + 1) * P])
        own = []
        for q in range(PARTS):
            cols = slice(q * P, (q + 1) * P)
            quantize(c1_w[:, cols], c_s[1][:, cols], c_parts[q])
            if q == 0:
                c0_w.append(keep.tile([P, HALF], U32, name="c0_w1", tag="c_part0", align_bytes=64))
                quantize(c0_w[1][:], c_s[0][:, HALF:J], c_bf0[:, PACK * HALF : PACK * J])
            c_words = (c0_w[q // 2][:, P * (q % 2) : P * (q % 2 + 1)], c1_w[:, cols])
            bank = psum.tile([P, PACK, P], F32, name=f"own{q}", tag=f"y{q}")
            for a in range(PASSES):
                for t in range(PACK):
                    nc.tensor.matmul_mx(
                        out=bank[:, t, :],
                        lhsT=wc_w[a][:, P * t : P * (t + 1)].bitcast(FP8X4),
                        lhsT_scale=wc_s[a][:, P * t : P * (t + 1)],
                        rhs=c_words[a].bitcast(FP8X4),
                        rhs_scale=c_s[a][:, cols],
                        start=(a == 0 and t == 0),
                        stop=(a == PASSES - 1 and t == PACK - 1),
                    )
            own.append(bank)

        out_rows = out.rearrange("(b p) j -> p b j", p=P)
        h_parts = []
        for q in range(PARTS):
            summed = keep.tile([P, PACK * P], BF16, name=f"summed{q}", tag=f"summed{q}")
            pooled = best[q // 2][:, :, P * (q % 2) : P * (q % 2 + 1), :]
            nc.vector.tensor_tensor(
                summed[:].rearrange("p (j u e) -> p j u e", u=2, e=2),
                own[q][:].rearrange("p (u e) j -> p j u e", e=2),
                pooled.rearrange("p u j e -> p j u e"),
                ALU.add,
            )
            h_bf = keep.tile([P, PACK * P], BF16, name=f"h_bf{q}", align_bytes=64)
            if q < PARTS - 1:
                nc.scalar.activation(out=h_bf[:], in_=summed[:], func=ACT.Relu)
            else:
                nc.vector.tensor_scalar_max(h_bf[:], summed[:], 0.0)
            h_parts.append(h_bf)

        def second_layer(q):
            h_w = keep.tile([P, P], U32, name=f"h_w{q}", align_bytes=64)
            h_s = keep.tile([P, P], U8, name=f"h_s{q}", align_bytes=64)
            quantize(h_w[:], h_s[:], h_parts[q][:])
            bank = psum.tile([P, N // P, P], F32, name=f"y{q}", tag=f"x{q}")
            for n in range(N // P):
                nc.tensor.matmul_mx(
                    out=bank[:, n, :],
                    lhsT=wd_w[:, P * n : P * (n + 1)].bitcast(FP8X4),
                    lhsT_scale=planes[:, n, WD_COL:PLANE],
                    rhs=h_w[:].bitcast(FP8X4),
                    rhs_scale=h_s[:],
                    start=True,
                    stop=True,
                )
            return bank

        late = keep.tile([P, PARTS - 1, N // P, P], F32, name="late_results", tag=f"summed{PARTS - 1}")

        def gate_and_store(q, bank):
            cols = slice(q * P, (q + 1) * P)
            res = keep.tile([P, N // P, P], F32, name="res0")[:] if q == 0 else late[:, q - 1]
            nc.vector.tensor_tensor(res, bank[:], gate[:, :, cols], ALU.mult)
            nc.sync.dma_start(out=out_rows[:, :, cols], in_=res)

        y = [second_layer(q) for q in range(PARTS)]
        for q in range(PARTS):
            gate_and_store(q, y[q])
